import numpy as np, ml_dtypes
CORES = [5,29,101,125,133,157,229,253]
N = 8
BF = ml_dtypes.bfloat16
def gentries(a):
    return np.ascontiguousarray(a.reshape(8, 16, -1).transpose(0, 2, 1)).reshape(8, -1)
def gtable(e):
    e = np.asarray(e); return np.ascontiguousarray(e.reshape(8, -1, 16).transpose(0, 2, 1)).reshape(128, -1).astype(np.int32)
W, L, S, ST = 2048, 256, 16, 5
def parts(rng):
    x = rng.integers(0, 64, (N, 8, 16, W)); v = rng.integers(0, W, (N, 8, L, S)); c = rng.integers(0, W, (N, 8, L, S))
    n = np.where(rng.random((N, 8, L)) < 0.4, rng.integers(0, 4, (N, 8, L)), rng.integers(4, S + 1, (N, 8, L)))
    return x, v, c, n, rng.integers(220, 460, (N, 8)), rng.integers(0, 256, (N, 8, 16))
def pack(x, v, c, n, th, w):
    return {"xc": np.ascontiguousarray(x.reshape(N, 128, W)).astype(np.float32).astype(BF), "vl": np.stack([gtable(a.reshape(8, -1)) for a in v]), "cl": np.stack([gtable(a.reshape(8, -1)) for a in c]),
            "ln": np.ascontiguousarray(n).astype(np.int32), "th": np.ascontiguousarray(th.reshape(N, 8, 1)).astype(np.int32), "wt": np.ascontiguousarray(w.reshape(N, 128, 1)).astype(np.int32)}
def setup_inputs(rng):
    return pack(*parts(rng))
def setup_inputs_ties(rng):
    x, v, c, n, th, w = parts(rng)
    x = np.repeat(8 * rng.integers(0, 8, (N, 8, 1, W)), 16, axis=2); up = rng.integers(0, 3, (N, 8, W)) * (rng.random((N, 8, W)) < 0.4)
    x = x + up[:, :, None, :] * (np.arange(16)[:, None] == rng.integers(0, 16, (N, 8, 1, W)))
    o = np.argsort(rng.random((N, 8)), axis=1); j = o >> 1; less = np.where(rng.random((N, 8)) < 0.6, rng.integers(0, 2, (N, 8)), rng.integers(0, 32, (N, 8)))
    th = np.maximum(128 * j - less, 0); s = np.arange(S)
    for r in range(N):
        z = 128 * int(rng.integers(4, 7))
        for g, e in ((int(np.argmin(o[r])), 0), (int(np.argmax(o[r])), 1)):
            th[r, g] = z + e
            x[r, g, :, 0] = 0; x[r, g, :, 1] = 56; x[r, g, :, 2] = z >> 4; x[r, g, int(rng.integers(0, 16)), 2] += 1
            v[r, g, 1::2] = np.where(s < 2, 0, 2); c[r, g, 1::2] = np.where(s < 1, 1, 2); n[r, g, 1::2] = rng.integers(4, S + 1, L // 2)
    q = int(rng.integers(0, N)); a = (q - 1) % N; b = (q - 2) % N
    n[a] = np.where(n[a] >= 4, rng.integers(4, 6, (8, L)), n[a])
    n[q] = rng.integers(0, 4, (8, L)); p = rng.permutation(8 * L)[:31]; one = rng.integers(0, W, (31, 1))
    n[q, p // L, p % L] = 4; v[q, p // L, p % L] = one; c[q, p // L, p % L] = one; th[q] = 128 * rng.integers(1, 4, 8) - 16
    x[b, :, :, 16:40:3] = 0; x[b, :, :, 17:40:3] = 56; x[b, :, :, 18:40:3] = 63; x[b, :, :, 64:128] = 8 * rng.integers(0, 2, (8, 1, 64))
    f0 = 16 + 3 * (np.arange(L // 4)[:, None] & 7); far = rng.integers(64, 128, (8, L // 4, S)); e = rng.integers(128, W, (8, L // 4, S))
    v[b, :, ::4] = np.where(s == 0, e, np.where((s == 1) | (s >= S - 3), f0 + 2, np.where(s == 2, f0 + 1, far)))
    c[b, :, ::4] = np.where(s == 0, f0 + 2, np.where((s == 1) | (s == S - 3), f0, rng.integers(128, W, far.shape)))
    n[b, :, ::4] = S
    return pack(x, v, c, n, th, w)
def setup_inputs_alike(rng):
    x, v, c, n, th, w = parts(rng)
    few = np.array([0, W - 1, W // 2, 3, W - 2, 17])
    v[:, ::2] = few[rng.integers(0, 6, (N, 4, L, S))]; v[:, 1::2, :, 0] = few[rng.integers(0, 6, (N, 4, L))]
    w[:, ::2] = 0; th[:, ::2] = rng.integers(0, 260, (N, 4)); th[:, 1::2] = rng.integers(150, 500, (N, 4))
    o = rng.permutation(4); shutting = 2 * int(o[0]); taking = 2 * int(o[1]); growing = 1 + 2 * int(rng.integers(0, 4))
    n[:, growing] = rng.integers(4, S + 1, (N, L)); v[:, growing, :, 0] = few[int(rng.integers(0, 6))]; th[:, growing] = 0
    n[:, shutting] = rng.integers(ST + 3, S + 1, (N, L)); th[:, shutting] = 1008
    rest = np.where(rng.random((N, L)) < 0.8, 0, rng.integers(1, 4, (N, L)))
    n[:, taking] = np.where(np.arange(N)[:, None] % 2 == 0, rng.integers(ST + 3, S + 1, (N, L)), rest); th[:, taking] = 1008
    return pack(x, v, c, n, th, w)
def setup_inputs_corners(rng):
    x, v, c, n, th, w = parts(rng)
    lo = (W - 1) * rng.integers(0, 2, (N, 8, 1)); hi = W - 1 - lo
    x[..., 0] = np.where(lo == 0, 0, 63); x[..., W - 1] = np.where(lo == 0, 63, 0)
    n = rng.choice(np.array([0, 1, 2, 3, 4, 5, S - 1, S]), (N, 8, L)); kind = rng.integers(0, 5, (N, 8, L))
    for g, i in ((0, 0), (7, L - 1)):
        n[0, g, i] = S; kind[0, g, i] = 0; n[1, g, i] = 0
    n[N - 1, 7, L - 2] = S; kind[N - 1, 7, L - 2] = 1
    s = np.arange(S); q = np.maximum(n, 4)[..., None]; kd = kind[..., None]; A = lo[..., None]; H = hi[..., None]
    v0 = np.where((s < 2) | (s == q - 1), H, A); v1 = np.where((s == q - 3) | (s == q - 2), H, A); v2 = np.where(s >= q - 3, H, A)
    one = rng.integers(0, W, (N, 8, L, 1))
    v = np.where(kd == 0, v0, np.where(kd == 1, v1, np.where(kd == 2, v2, np.where(kd == 3, one, v))))
    c = np.where(kd < 3, A, np.where(kd == 3, one, c))
    v = np.where(s < n[..., None], v, (W - 1) * rng.integers(0, 2, v.shape)); c = np.where(s < n[..., None], c, (W - 1) * rng.integers(0, 2, c.shape))
    return pack(x, v, c, n, np.array([0, 5, 500, 900])[np.argsort(rng.random((N, 8)), axis=1) >> 1], w)
def setup_inputs_ends(rng):
    x, v, c, n, th, w = parts(rng)
    e = 63 * rng.integers(0, 2, (N, 8, 1)); e[N - 1, 7] = 0
    x = 63 * rng.integers(0, 2, (N, 8, 16, W)); x[..., 0] = e; x[..., W - 1] = 63 - e
    for j in range(1, 17):
        for col in (j, W - 1 - j):
            x[..., col] = 63 - e; x[:, :, j - 1, col] = np.abs(62 - e[..., 0])
    v = np.where(rng.random(v.shape) < 0.75, (W - 1) * rng.integers(0, 2, v.shape), v); c = np.where(rng.random(c.shape) < 0.75, (W - 1) * rng.integers(0, 2, c.shape), c)
    kind = rng.integers(0, 3, (N, 8, L)); kind[..., 0] = 1; kind[..., L - 1] = 1; kind[..., 1] = 2; kind[..., L - 2] = 2
    k1 = kind == 1; k2 = kind == 2; v[k1 | k2] = W - 1; c[k1] = W - 1
    c = np.where(k2[..., None], (W - 1) * rng.integers(0, 2, c.shape), c)
    near = rng.integers(1, 17, (N, 8, L)); near = np.where(rng.random((N, 8, L)) < 0.5, near, W - 1 - near)
    v[..., 0] = np.where(k1, near, v[..., 0]); c[..., 0] = np.where(k1, 0, c[..., 0]); c[..., S - 3] = np.where(k1 | k2, 0, c[..., S - 3])
    v[..., S - 1] = np.where(k1, (W - 1) * rng.integers(0, 2, (N, 8, L)), v[..., S - 1]); v[N - 1, 7, L - 1, S - 1] = 0
    n = np.where(rng.random((N, 8, L)) < 0.7, S, 0); n[..., 0] = S; n[..., 1] = S; n[..., 2] = 0; n[..., L - 2] = S; n[..., L - 1] = S; n[0, :, L - 1] = 0
    th = 1008 * (np.argsort(rng.random((N, 8)), axis=1) & 1)
    if th[N - 1, 7] > 0: th[N - 1] = 1008 - th[N - 1]
    w = 255 * rng.integers(0, 2, (N, 8, 16)); w[:, 7] = 255; w[:, 0] = 0
    return pack(x, v, c, n, th, w)
def setup_inputs_spread(rng):
    x, v, c, n, th, w = parts(rng)
    x = np.minimum((np.exp2(6.1 * rng.random((N, 8, 1, W))) * rng.random((N, 8, 16, W))).astype(np.int64), 63)
    po = rng.choice(np.array([1.0, 2.0, 4.0]), (N, 8, 1, 1)); v = np.minimum((W * rng.random(v.shape) ** po).astype(np.int64), W - 1); c = np.minimum((W * rng.random(c.shape) ** po[:, ::-1]).astype(np.int64), W - 1)
    n = np.minimum(((S + 1) * rng.random((N, 8, L)) ** rng.choice(np.array([0.5, 1.0, 2.0]), (N, 8, 1))).astype(np.int64), S)
    th = np.minimum(np.exp2(10 * rng.random((N, 8))).astype(np.int64) - 1, 1008); w = np.minimum(np.exp2(8.05 * rng.random((N, 8, 16))).astype(np.int64) - 1, 255)
    return pack(x, v, c, n, th, w)
def check_inputs(d):
    bad = []
    for k, lo, hi in (("xc", 0, 63), ("vl", 0, W - 1), ("cl", 0, W - 1), ("ln", 0, S), ("th", 0, 1008), ("wt", 0, 255)):
        a = np.asarray(d[k]).astype(np.float64)
        if not (np.min(a) >= lo and np.max(a) <= hi): bad.append("range of " + k)
    a = np.asarray(d["xc"]).astype(np.float64)
    if not np.all(np.floor(a) == a): bad.append("xc is not whole")
    return bad
def reference(xc, vl, cl, ln, th, wt):
    X = np.ascontiguousarray(xc.astype(np.float32).astype(np.int32).reshape(N, 8, 16, W).transpose(0, 1, 3, 2))
    V = np.stack([gentries(q) for q in vl]).astype(np.int32).reshape(N, 8, L, S); C = np.stack([gentries(q) for q in cl]).astype(np.int32).reshape(N, 8, L, S)
    n = ln.astype(np.int64).reshape(N, 8, L); lim = th.astype(np.int64).reshape(N, 8, 1, 1); w = wt.astype(np.int64).reshape(N, 8, 1, 16)
    a = np.arange(N)[:, None, None, None]; b = np.arange(8)[None, :, None, None]; s = np.arange(S); shut = np.zeros(N, np.int64)
    for t in range(ST):
        XV = X[a, b, V]; XC = X[a, b, C]; live = n >= 4
        bend = np.add.reduce(np.abs(XV[:, :, :, :-1] + XV[:, :, :, 1:] - 2 * XC[:, :, :, :-1]), axis=-1, dtype=np.int32)
        k = np.argmax(np.where(s[:-1] <= n[..., None] - 3, bend, -1), axis=3)[..., None]
        Vk = np.take_along_axis(V, k, 3); Vn = np.take_along_axis(V, k + 1, 3); Ck = np.take_along_axis(C, k, 3)
        y = np.clip(X[a, b, Vk] + X[a, b, Vn] - X[a, b, Ck], 0, 63)
        dist = np.add.reduce(np.abs(XV - y), axis=-1, dtype=np.int32)
        fit = (s >= k + 2) & (s <= n[..., None] - 1) & (dist <= lim + shut[:, None, None, None]) & live[..., None]
        close = np.any(fit, axis=3); m = np.argmax(fit, axis=3)[..., None]; grow = live & ~close
        size = np.where(close[..., None], m - k - 1, 0)
        ix = np.minimum(k + 1 + s, S - 1); keep = s < size
        PV = np.where(keep, np.take_along_axis(V, ix, 3), 0); PC = np.where(keep, np.take_along_axis(C, ix, 3), 0)
        y = y[:, :, :, 0]; u = np.add.reduce(w * y, axis=-1) & (W - 1)
        h = (((u * u) >> 5) + 37 * Vk[..., 0].astype(np.int64)) & (W - 1)
        src = np.minimum(np.where(s <= k, s, s + size - grow[..., None].astype(np.int64)), S - 1)
        V2 = np.take_along_axis(V, src, 3); C2 = np.take_along_axis(C, src, 3); new = grow[..., None] & (s == k + 1)
        V2 = np.where(new, h[..., None], V2); C2 = np.where(new, Vk, np.where(live[..., None] & (s == k), Vn, C2))
        n2 = np.minimum(n + grow.astype(np.int64), S) - size[..., 0]
        for i in range(L - 1, -1, -1):
            p, q = np.nonzero(grow[:, :, i]); X[p, q, h[p, q, i]] = y[p, q, i]
        d = 1 + t % (N - 1)
        came = np.roll(size, d, axis=0)[..., 0]; yin = np.roll(y, d, axis=0); lin = np.roll(live, d, axis=0)
        take = ~live & (came > n)
        V = np.where(take[..., None], np.roll(PV, d, axis=0), V2); C = np.where(take[..., None], np.roll(PC, d, axis=0), C2); n = np.where(take, came, n2)
        V = np.where(s < n[..., None], V, 0).astype(np.int32); C = np.where(s < n[..., None], C, 0).astype(np.int32)
        has = lin & (n >= 1); old = X.copy()
        for i in range(L - 1, -1, -1):
            p, q = np.nonzero(has[:, :, i]); z = V[p, q, i, 0]; X[p, q, z] = (old[p, q, z] + yin[p, q, i]) >> 1
        shut = np.add.reduce(close.astype(np.int64).reshape(N, -1), axis=1) & 31
    return {"yx": np.ascontiguousarray(X.transpose(0, 1, 3, 2)).reshape(N, 128, W).astype(np.float32).astype(BF), "yv": np.stack([gtable(q.reshape(8, -1)) for q in V]).astype(np.float32),
            "yc": np.stack([gtable(q.reshape(8, -1)) for q in C]).astype(np.float32), "yn": n.astype(np.float32)}

@@ -1,0 +1,718 @@
+import numpy as np
+from concourse.mybir import dt, AluOpType as A, AxisListType, ActivationFunctionType as F
+
+ST = 5
+B2, F4, I4, U2 = "bfloat16", "float32", "int32", "uint16"
+SCRATCH = {}
+
+
+SHAPE = {}
+PLACE = {}
+
+
+def _sb(name, shape, dtype, where="sbuf"):
+    SCRATCH[name] = (where, shape, dtype)
+    SHAPE[name] = shape
+
+
+def _pack(name, width, dtype):
+    box = "box_" + dtype
+    at = SCRATCH[box][1][1] if box in SCRATCH else 0
+    SCRATCH[box] = ("sbuf", [128, at + (width + 15) // 16 * 16], dtype)
+    SHAPE[name] = [128, width]
+    PLACE[name] = (box, at)
+
+
+for _n, _w in (("X", 2304), ("XV", 4112), ("XC", 4096), ("WIN0", 8720), ("WIN1", 8720), ("E", 2048), ("Ev", 2048), ("Ec", 2048),
+               ("wE", 2048), ("Rhi", 2048), ("Rlo", 2048), ("NBm", 2048), ("ID", 128), ("NEGI", 128), ("NEG2", 128), ("BO", 128),
+               ("RV0", 128), ("RV1", 128), ("RS0", 128), ("RS1", 128), ("D01", 128), ("S23", 128), ("REPv", 128), ("ONES", 128),
+               ("RB", 256), ("SEEDP", 256), ("SEEDG", 256), ("SEEDN", 256), ("SEEDS", 256), ("SHS", 256), ("LChi", 256), ("LClo", 256),
+               ("Q0T", 256), ("M1", 256), ("M2", 256), ("PRE", 256), ("SK", 256), ("OH", 256), ("OHG", 256), ("GT", 256), ("SH", 256),
+               ("NS", 256), ("NF", 256), ("MS", 256), ("G1", 256), ("G2", 256), ("G3", 256), ("YT", 256), ("PG1", 256), ("PG2", 256),
+               ("P0", 256), ("CB", 256), ("BS", 256), ("BT", 256), ("N192", 256), ("ZERO", 256), ("LNB", 258), ("HHL", 32), ("CLB", 1)):
+    (_pack if _w <= 258 else lambda n, w, d: _sb(n, [128, w], d))(_n, _w, B2)
+for _n, _w in (("CC", 16), ("KM", 256), ("RF", 256), ("POS0", 256), ("POS1", 256), ("II", 256), ("TPk0", 256), ("TPk1", 256),
+               ("TPn0", 256), ("TPn1", 256), ("IC", 16), ("DD", 16), ("OHT", 256), ("OHPP", 256), ("SRC", 256), ("NN", 16), ("LIVE", 16),
+               ("NR", 16), ("CL", 16), ("GR", 16), ("Ta", 16), ("Tb", 16), ("Td", 16), ("Te", 16), ("QM", 16), ("QN", 16),
+               ("TK", 16), ("HE", 16), ("HF", 16), ("HG", 16), ("HD", 16), ("VG", 16), ("HAS", 16), ("lim", 1), ("thc", 1), ("cls", 1),
+               ("t1", 16), ("FIN", 256), ("VMV", 256), ("VMC", 256), ("AL", 256)):
+    _pack(_n, _w, F4)
+_sb("ON", [128, 256], F4)
+for _n, _w in (("VI", 512), ("LNI", 257), ("WTI", 1)):
+    _sb(_n, [128, _w], I4)
+for _n, _w in (("VJ", 512), ("VL", 512), ("im", 128), ("imh", 128), ("ip", 1), ("ii", 8),
+               ("J32", 2048), ("KI", 16), ("OFI", 16), ("QK", 16), ("OF0", 16), ("UI", 16), ("SQ", 16), ("HI", 16), ("HP", 32), ("ci", 1)):
+    _pack(_n, _w, I4)
+for _n, _w in (("VU", 256), ("CU", 256), ("OFU", 16), ("OFP", 16), ("OFH", 16), ("OFB", 16), ("V0U", 16), ("S0U", 16), ("SRCU", 256),
+               ("HR", 256), ("VR", 256)):
+    _pack(_n, _w, U2)
+_sb("HL", [128, 4, 8, 2, 16], B2)
+_sb("FT", [128, 8, 2, 16], F4)
+_sb("FO0", [128, 8, 2, 16], F4)
+_sb("FO1", [128, 8, 2, 16], F4)
+_sb("FD", [128, 4, 128], F4)
+_sb("EQ", [128, 16, 256], B2)
+_sb("Z", [128, 16, 256], B2)
+_sb("Z2", [128, 16, 256], B2)
+for _t in range(ST):
+    _sb("YM%d" % _t, [128, 272], B2)
+    _sb("YR%d" % _t, [128, 272], B2)
+    _sb("SM%d" % _t, [128, 32], B2)
+    _sb("SR%d" % _t, [128, 32], B2)
+    _sb("PD%d" % _t, [128, 1024], B2, "dram")
+    _sb("PI%d" % _t, [128, 1024], B2, "dram")
+for _t in range(4):
+    _sb("PZ%d" % _t, [128, 2, 256], F4, "psum")
+for _n in ("PK", "PQ", "PS", "PT"):
+    _sb(_n, [128, 512], F4, "psum")
+SEMAPHORES = ["q_pe", "q_dve", "q_act", "q_g", "loc", "dv", "dc", "dx", "dln", "dwt", "pst", "dout"]
+for _t in range(ST):
+    SEMAPHORES += ["po%d" % _t, "pi%d" % _t, "am%d" % _t, "ay%d" % _t, "as%d" % _t]
+
+_RANGE = {}
+
+
+def _span(name, idx):
+    key = name + repr(idx)
+    if key not in _RANGE:
+        shape = SHAPE[name][1:]
+        a = np.arange(int(np.prod(shape))).reshape(shape)[idx]
+        _RANGE[key] = (int(a.min()), int(a.max()) + 1)
+    return _RANGE[key]
+
+
+def _queues(g, core, T):
+    eng = {"pe": g.tensor, "dve": g.vector, "act": g.scalar, "g": g, "sp": g.sync}
+    cnt = {"pe": 0, "dve": 0, "act": 0, "g": 0}
+    known = {q: {} for q in eng}
+    vc, recs, total = {}, {}, {}
+
+    def V(name, *idx):
+        lo, hi = _span(name, idx) if idx else (0, 1 << 20)
+        if name in PLACE:
+            box, at = PLACE[name]
+            k = idx[0] if idx else slice(0, SHAPE[name][1])
+            return (T[box][:, at + k.start:at + k.stop:k.step or 1], name, lo, hi)
+        return (T[name][(slice(None),) + idx] if idx else T[name][:], name, lo, hi)
+
+    def deps(q, outs, ins, own=None):
+        need = {}
+        for lst, wr in ((ins, 0), (outs, 1)):
+            for (_, name, lo, hi) in lst:
+                psum = SCRATCH.get(name, ("",))[0] == "psum"
+                for r in recs.get(name, ()):
+                    if (q == "pe" and r[4] == "pe") or r[3][0] == own:
+                        continue
+                    if psum and r[4] != q:
+                        hit = True
+                    else:
+                        hit = r[0] < hi and lo < r[1] and (r[2] or wr)
+                    if hit:
+                        s, v = r[3]
+                        if known[q].get(s, 0) < v and need.get(s, 0) < v:
+                            need[s] = v
+        for s in sorted(need):
+            for s2, v2 in need.items():
+                if s2 != s and vc.get((s2, v2), {}).get(s, 0) >= need[s]:
+                    need[s] = 0
+        for s in sorted(need):
+            v = need[s]
+            if v:
+                eng[q].wait_ge(T.sem[s], v)
+                known[q][s] = v
+                for s2, v2 in vc.get((s, v), {}).items():
+                    if known[q].get(s2, 0) < v2:
+                        known[q][s2] = v2
+
+    def note(q, tok, outs, ins):
+        for (_, name, lo, hi) in ins:
+            l = recs.setdefault(name, [])
+            l[:] = [r for r in l if not (not r[2] and r[4] == q and lo <= r[0] and r[1] <= hi)]
+            l.append((lo, hi, 0, tok, q))
+        for (_, name, lo, hi) in outs:
+            l = recs.setdefault(name, [])
+            psum = SCRATCH.get(name, ("",))[0] == "psum"
+            l[:] = [r for r in l if not (lo <= r[0] and r[1] <= hi) or (psum and r[4] != q)]
+            if psum:
+                l[:] = [r for r in l if r[4] == q] + [r for r in l if r[4] != q and known[q].get(r[3][0], 0) < r[3][1]]
+            l.append((lo, hi, 1, tok, q))
+
+    def run(q, call, outs, ins):
+        deps(q, outs, ins)
+        cnt[q] += 1
+        s = "q_" + q
+        call(eng[q]).then_inc(T.sem[s], 1)
+        tok = (s, cnt[q])
+        d = dict(known[q])
+        d[s] = cnt[q]
+        vc[tok] = d
+        note(q, tok, outs, ins)
+
+    def dma(q, sem, n, out, in_):
+        deps(q, [out], [in_], sem)
+        eng[q].dma_start(out[0], in_[0]).then_inc(T.sem[sem], 16)
+        total[sem] = n
+        vc.setdefault((sem, n), dict(known[q]))
+        note("dma", (sem, n), [out], [in_])
+
+    def arrive(name, sem, n):
+        total[sem] = n
+        note("ext", (sem, n), [(None, name, 0, 1 << 20)], [])
+
+    def before(q, ins):
+        deps(q, [], ins)
+
+    def finish():
+        for q in cnt:
+            if cnt[q] and known["g"].get("q_" + q, 0) < cnt[q]:
+                g.wait_ge(T.sem["q_" + q], cnt[q])
+        for s in sorted(total):
+            if known["g"].get(s, 0) < total[s]:
+                g.wait_ge(T.sem[s], total[s])
+
+    return V, run, dma, arrive, before, finish, total
+
+
+def _send(core, T, topo, g, out, in_, arrived, dst):
+    e = topo.engines(core, dst)[:8]
+    rid, pid = topo.addr(dst, core)
+    g.remote_dma(out, in_, T.sem[arrived], T.sem["loc"], pid, rid, sum(1 << k for k in e))
+    return len(e)
+
+
+def _relays(core, dst, topo):
+    if topo.may_write(core, dst):
+        return []
+    c = [k for k in topo.cores_of(core) if k != core and topo.may_write(k, dst)]
+    c.sort(key=lambda k: (topo.die(k) != topo.die(core), k))
+    return [c[0], c[1 % len(c)]]
+
+
+def _relay_program(g, core, T, topo):
+    loc = 0
+    for t in range(ST):
+        for r, src in enumerate(T.cores):
+            dst = T.cores[(r + 1 + t % 7) % len(T.cores)]
+            rl = _relays(src, dst, topo)
+            if core not in rl:
+                continue
+            n = len(topo.engines(src, core)[:8])
+            for k, (name, sem) in enumerate((("PI", "am"), ("YR", "ay"), ("SR", "as"))):
+                if rl[0 if k == 0 else 1] == core:
+                    g.wait_ge(T.sem[sem + str(t)], n)
+                    loc += _send(core, T, topo, g, T[name + str(t)][:], T[name + str(t)][:], sem + str(t), dst)
+    if loc:
+        g.wait_ge(T.sem["loc"], loc)
+
+
+def rank_program(g, core, T, topo):
+    rank = T.rank_of(core)
+    if rank is None:
+        return _relay_program(g, core, T, topo)
+    V, run, dma, arrive, before, finish, total = _queues(g, core, T)
+    n_loc = [0]
+    sl = slice
+    X_ALL, X_WIN = (sl(0, 2304),), (sl(0, 2048),)
+
+    def mm(out, lhsT, rhs, a, z):
+        run("pe", lambda e: e.matmul(out[0], lhsT[0], rhs[0], a, z), [out], [lhsT, rhs])
+
+    def ts(out, in0, s1, op0, s2=None, op1=None):
+        ins = [in0] + [s for s in (s1, s2) if isinstance(s, tuple)]
+        a1 = s1[0] if isinstance(s1, tuple) else s1
+        a2 = s2[0] if isinstance(s2, tuple) else s2
+        if op1 is None:
+            run("dve", lambda e: e.tensor_scalar(out[0], in0[0], a1, None, op0), [out], ins)
+        else:
+            run("dve", lambda e: e.tensor_scalar(out[0], in0[0], a1, a2, op0, op1), [out], ins)
+
+    def tt(out, a, b, op):
+        run("dve", lambda e: e.tensor_tensor(out[0], a[0], b[0], op), [out], [a, b])
+
+    def tc(out, in_):
+        run("dve", lambda e: e.tensor_copy(out[0], in_[0]), [out], [in_])
+
+    def ac(out, in_, f=F.Copy, scale=1.0):
+        ins = [in_] + ([scale] if isinstance(scale, tuple) else [])
+        sc = scale[0] if isinstance(scale, tuple) else scale
+        run("act", lambda e: e.activation(out[0], in_[0], f, scale=sc), [out], ins)
+
+    def scan(out, d0, d1, op0, op1):
+        run("dve", lambda e: e.tensor_tensor_scan(out[0], d0[0], d1[0], 0.0, op0, op1), [out], [d0, d1])
+
+    def fill(out, c):
+        run("dve", lambda e: e.memset(out[0], c), [out], [])
+
+    def iota(out, pattern, base=0, cm=0):
+        run("g", lambda e: e.iota(out[0], pattern, base, cm, allow_small_or_imprecise_dtypes=True), [out], [])
+
+    def gather(q, out, win, off):
+        ap = win[0].indirect(off[0])
+        if q == "act":
+            run("act", lambda e: e.activation(out[0], ap, F.Copy), [out], [win, off])
+        else:
+            run("dve", lambda e: e.tensor_copy(out[0], ap), [out], [win, off])
+
+    def col(k):
+        return V("CC", sl(k, k + 1))
+
+    def small(out, mats, rhs_name, n16):
+        for b in range(16):
+            mm(out, V(mats, sl(b * 128, b * 128 + 128)), V(rhs_name, sl(b, n16, 16)), b == 0, b == 15)
+
+    AND, SHR = A.bitwise_and, A.arith_shift_right
+
+    dma("sp", "dv", 16, V("VI", sl(0, 256)), (T["vl"][:], "vl", 0, 1))
+    dma("sp", "dc", 16, V("VI", sl(256, 512)), (T["cl"][:], "cl", 0, 1))
+    dma("sp", "dx", 16, V("X", sl(0, 2048)), (T["xc"][:], "xc", 0, 1))
+    dma("sp", "dwt", 16, V("WTI"), (T["wt"][:], "wt", 0, 1))
+    fill(V("LNI"), 0)
+    for out_sl, nm in ((sl(0, 256), "ln"), (sl(256, 257), "th")):
+        o = V("LNI", out_sl)
+        dma("sp", "dln", 32, (T["LNI"][0:128:16, out_sl], "LNI", o[2], o[3]), (T[nm][:], nm, 0, 1))
+    iota(V("im"), [[1, 128]])
+    iota(V("ip"), [[0, 1]], 0, 1)
+    iota(V("LClo"), [[0, 16], [16, 16]])
+    iota(V("LChi"), [[256, 16], [0, 16]])
+    iota(V("IC"), [[16, 16]])
+    iota(V("II"), [[16, 16], [0, 16]])
+    iota(V("POS0"), [[16, 16], [-256, 16]], 3840)
+    iota(V("POS1"), [[256, 16], [16, 16]])
+    iota(V("RF"), [[0, 16], [1, 16]])
+    iota(V("WIN0", sl(0, 4368)), [[0, 4368]])
+    iota(V("J32"), [[16, 8], [0, 16], [1, 16]])
+
+    i_ = lambda k: V("ii", sl(k, k + 1))
+    ts(i_(0), V("ip"), 15, AND)
+    ts(i_(1), V("ip"), 4, SHR)
+    ts(i_(2), V("ip"), 31, AND)
+    ts(i_(3), V("ip"), 4, SHR, 1, AND)
+    tc(col(0), V("ip"))
+    ts(V("imh"), V("im"), 4, SHR)
+    tc(V("CC", sl(1, 3)), V("ii", sl(0, 2)))
+    tc(col(4), i_(3))
+    ts(col(3), i_(3), -1.0, A.mult, 1.0, A.add)
+    ts(col(5), i_(0), -2.0, A.mult, 15.0, A.add)
+    ts(col(6), i_(2), -2.0, A.mult, 31.0, A.add)
+    ts(V("ID"), V("im"), col(0), A.is_equal)
+    ts(V("CC", sl(5, 7)), V("CC", sl(5, 7)), col(0), A.add)
+    ts(V("BO"), V("imh"), col(2), A.is_equal)
+    ts(col(7), i_(0), 1.5, A.is_le)
+    ts(col(8), i_(0), 3.5, A.is_le)
+    for nm, c, h in (("RV0", 5, 3), ("RV1", 5, 4), ("RS0", 6, 3), ("RS1", 6, 4)):
+        ts(V(nm), V("im"), col(c), A.is_equal, col(h), A.mult)
+    tt(col(8), col(8), col(7), A.subtract)
+    ts(V("NEG2"), V("im"), col(0), A.is_equal, -2.0, A.mult)
+    fill(V("E"), 0.0)
+    for k in range(2):
+        h = sl(256 * k, 256 * k + 256)
+        ts(V("VJ", h), V("VI", h), 1792, AND)
+        ts(V("VL", h), V("VI", h), 255, AND)
+        tc(V("HL", 2 * k, sl(0, 8), sl(0, 2), sl(0, 16)), V("VJ", h))
+        tc(V("HL", 2 * k + 1, sl(0, 8), sl(0, 2), sl(0, 16)), V("VL", h))
+    for a in range(4):
+        dma("sp", "pst", 64, (T["PD0"][32 * a:32 * a + 32, :], "PD0", 1024 * a, 1024 * a + 1024), V("HL", a, sl(0, 8), sl(0, 2), sl(0, 16)))
+    for a in range(4):
+        dma("sp", "po0", 64, (T["WIN0"][a:128:16, 16:4112], "WIN0", 16, 4112), (T["PD0"][32 * a:32 * a + 32, :], "PD0", 1024 * a, 1024 * a + 1024))
+    for k, dst in enumerate(("VU", "CU")):
+        pz = "PZ%d" % k
+        for kap in range(2):
+            o = V(pz, 0, sl(kap * 128, kap * 128 + 128))
+            for n in range(4):
+                part, sw = n // 2, n % 2
+                mm(o, V(("RV%d", "RS%d")[sw] % kap), V("HL", 2 * k + part, sl(0, 8), (kap, 1 - kap)[sw], sl(0, 16)), n == 0, n == 3)
+        for kap in range(2):
+            tc(V("FT", sl(0, 8), kap, sl(0, 16)), V(pz, 0, sl(kap * 128, kap * 128 + 128)))
+        tc(V("FIN"), V("FT", sl(0, 8), sl(0, 2), sl(0, 16)))
+        run("dve", lambda e: e.transpose(V("VMV")[0], V("FIN")[0]), [V("VMV")], [V("FIN")])
+        tc(V(dst), V("VMV"))
+    fill(V("XV", sl(0, 16)), 0.0)
+
+    def consts_early():
+        for k in range(8):
+            tc(V("E", sl(16 * k, 2048, 129)), V("BO", sl(16 * k, 16 * k + 16)))
+        fill(V("RB"), 1.0)
+        fill(V("RB", sl(0, 256, 16)), 0.0)
+        fill(V("SEEDS"), 1.0)
+        lengths_in()
+        start_step(0)
+        fill(V("Z", sl(0, 16), sl(0, 32)), 0.0)
+        fill(V("Q0T"), 0.0)
+        fill(V("Q0T", sl(0, 256, 16)), 16777216.0)
+        ts(V("LClo"), V("LClo"), col(1), A.add)
+
+    def consts_mid():
+        ts(V("PS", sl(256, 512)), V("RF"), col(1), A.is_gt)
+        tc(V("RF"), V("RB"))
+        ts(V("NEGI"), V("im"), col(0), A.is_equal, -1.0, A.mult)
+        fill(V("SEEDP"), -1.0)
+        fill(V("SEEDP", sl(1, 256, 16)), -65.0)
+        for nm in ("POS0", "POS1", "II", "IC"):
+            ts(V(nm), V(nm), col(1), A.add)
+        ts(V("D01"), V("im"), col(0), A.is_equal, col(7), A.mult)
+        tt(col(10), col(0), col(0), A.subtract)
+        ts(col(10), col(10), 2.0, A.add, col(0), A.add)
+        ts(V("S23"), V("im"), col(10), A.is_equal, col(7), A.mult)
+        ts(V("REPv"), V("BO"), col(7), A.mult)
+        ts(V("NBm"), V("J32"), col(0), A.is_equal, -1.0, A.mult)
+        fill(V("Z2", sl(0, 16), sl(224, 256)), 0.0)
+        tc(col(9), V("WTI"))
+        fill(V("Rhi"), 0.0)
+        fill(V("Rlo"), 0.0)
+        for k in range(8):
+            tc(V("Rhi", sl(16 * k, 2048, 128)), V("ID", sl(16 * k, 16 * k + 16)))
+            tc(V("Rlo", sl(16 * k + 1, 2048, 128)), V("ID", sl(16 * k, 16 * k + 16)))
+
+    def places(m, grow):
+        tt(V("OHT"), V("II"), V("POS%d" % m), A.subtract)
+        ts(V("TPk%d" % m), V("OHT"), 8192.0, A.add)
+        ts(V("TPn%d" % m), V("OHT"), 8448.0 - grow, A.add)
+
+    def consts_late():
+        ts(V("wE"), V("E"), col(9), A.mult)
+        ts(V("DD"), V("IC"), 2048.0, A.add)
+        places(0, -256.0)
+        fill(V("SEEDG"), -1.0)
+        fill(V("SEEDG", sl(1, 256, 16)), -65.0)
+        fill(V("ZERO"), 0.0)
+        fill(V("ONES"), 1.0)
+
+    def consts_last():
+        fill(V("SEEDN"), -0.0625)
+        fill(V("SEEDN", sl(1, 256, 16)), 3.9375)
+        fill(V("SHS"), 0.0)
+        fill(V("N192"), -192.0)
+        fill(V("WIN1", sl(0, 16)), 0.0)
+        places(1, 16.0)
+
+    def lengths_in():
+        tc(V("LNB", sl(0, 256)), V("LNI", sl(0, 256)))
+        ts(V("ci"), V("LNI", sl(256, 257)), 1016, AND)
+        tc(V("LNB", sl(256, 257)), V("ci"))
+        ts(V("ci"), V("LNI", sl(256, 257)), 7, AND)
+        tc(V("LNB", sl(257, 258)), V("ci"))
+        small(V("PS", sl(80, 96)), "E", "LNB", 256)
+        mm(V("PS", sl(96, 97)), V("BO"), V("LNB", sl(256, 257)), True, False)
+        mm(V("PS", sl(96, 97)), V("BO"), V("LNB", sl(257, 258)), False, True)
+        tc(V("NN"), V("PS", sl(80, 96)))
+        tc(V("thc"), V("PS", sl(96, 97)))
+        tc(V("lim"), V("thc"))
+
+    def start_step(t):
+        ts(V("LIVE"), V("NN"), 3.5, A.is_ge)
+        tt(V("Tb"), V("NN"), V("LIVE"), A.mult)
+        ts(V("SEEDS", sl(0, 256, 16)), V("Tb"), -15.0, A.add)
+        scan(V("NS"), V("RB"), V("SEEDS"), A.mult, A.add)
+        ts(V("M1"), V("NS"), 3.0, A.is_lt, -16777216.0, A.mult)
+        ts(V("M2"), V("NS"), 0.5, A.is_le, 8192.0, A.mult)
+        tc(V("YM%d" % t, sl(256, 272)), V("LIVE"))
+
+    def push(t, name, out_name, sem, via):
+        dst = T.cores[(rank + 1 + t % 7) % len(T.cores)]
+        rl = _relays(core, dst, topo)
+        to = rl[via] if rl else dst
+        before("g", [V(name)])
+        n_loc[0] += _send(core, T, topo, g, T[out_name][:], T[name][:], sem, to)
+        total["loc"] = n_loc[0]
+
+    def came(t, name, sem):
+        src = T.cores[(rank - 1 - t % 7) % len(T.cores)]
+        rl = _relays(src, core, topo)
+        arrive(name + str(t), sem + str(t), len(topo.engines(rl[0] if rl else src, core)[:8]))
+
+    def dedupe(vict, val1, act, vald, off, cb, meanwhile):
+        tt(V("HE"), val1, act, A.mult)
+        mm(V("PT", sl(256, 512)), V("BO"), V("ZERO"), True, False)
+        for c in range(16):
+            ts(V("EQ", c, sl(0, 256 - 16 * c)), V(vict, sl(16 * c, 256)), V("HE", sl(c, c + 1)), A.is_equal)
+            if c < 15:
+                mm(V("PT", sl(272 + 16 * c, 512)), V("BO"), V("EQ", c, sl(16, 256 - 16 * c)), False, False)
+        d = V("EQ", sl(0, 16), sl(0, 16))
+        tt(d, d, V("PS", sl(256, 512)), A.mult)
+        mm(V("PT", sl(256, 512)), V("BO"), d, False, True)
+        tt(V("Te"), vald, act, A.mult)
+        if cb == "act":
+            ac(V("CB"), V("PT", sl(256, 512)))
+        else:
+            tc(V("CB"), V("PT", sl(256, 512)))
+        small(V("PS", sl(32, 48)), "E", "CB", 256)
+        meanwhile()
+        ts(V("Td"), V("PS", sl(32, 48)), 0.5, A.is_lt)
+        tt(V("Td"), V("Td"), V("Te"), A.mult)
+        tt(V("t1"), V("Td"), V("DD"), A.add)
+        tc(V(off), V("t1"))
+
+    for t in range(ST):
+        cur, nxt = "WIN%d" % (t % 2), "WIN%d" % (1 - t % 2)
+        md = min(t, 1)
+        unit = (256.0, -16.0)[md]
+        S = str(t)
+        ym, sm = "YM" + S, "SM" + S
+
+        def gv(j):
+            for k in ((0,), (1,), (2, 3), ())[j] if t else ():
+                tc(V("VU", sl(64 * k, 64 * k + 64)), V("PZ%d" % k, 0, sl(0, 64)))
+                tc(V("CU", sl(64 * k, 64 * k + 64)), V("PZ%d" % k, 1, sl(0, 64)))
+            gather("dve", V("XV", sl(16 + 1024 * j, 16 + 1024 * j + 1024)), V("X", *X_WIN), V("VU", sl(64 * j, 64 * j + 64)))
+
+        def gc(q, u, n):
+            gather(q, V("XC", sl(512 * u, 512 * u + 512 * n)), V("X", *X_WIN), V("CU", sl(32 * u, 32 * u + 32 * n)))
+
+        def bend(u):
+            pz = "PZ%d" % (u % 4)
+            for k in range(2):
+                o = (2 * u + k) * 256
+                for src, mat, a in (("XV", "ID", 16 + o + 32), ("XV", "ID", o + 32), ("XC", "NEG2", o + 32)):
+                    mm(V(pz, k, sl(32, 256)), V(mat), V(src, sl(a, a + 224)), a == 16 + o + 32, src == "XC")
+            ac(V("Z", sl(2 * u, 2 * u + 2), sl(32, 256)), V(pz, sl(0, 2), sl(32, 256)), F.Abs, 4096.0)
+
+        def key(j):
+            o = V("PK", sl(64 * j, 64 * j + 64))
+            for k, m in enumerate(("M1", "Q0T", "LChi", "LClo")):
+                mm(o, V("ID"), V(m, sl(64 * j, 64 * j + 64)), k == 0, False)
+            for b in range(16):
+                mm(o, V("E", sl(b * 128, b * 128 + 128)), V("Z", sl(4 * j, 4 * j + 4), sl(b, 256, 16)), False, b == 15)
+
+        if t:
+            for a in range(4):
+                dma("sp", "po" + S, 64, (T["PD" + S][32 * a:32 * a + 32, :], "PD" + S, 1024 * a, 1024 * a + 1024), (T[cur][a:128:16, 16:4112], cur, 16, 4112))
+        push(t, "PD" + S, "PI" + S, "am" + S, 0)
+        if t == 0:
+            iota(V("WIN0", sl(4368, 8208)), [[0, 3840]])
+        gv(0)
+        gc("act", 0, 2)
+        if t == 0:
+            consts_early()
+        gv(1)
+        gc("act", 2, 2)
+        bend(0)
+        bend(1)
+        gv(2)
+        gc("act", 4, 2)
+        bend(2)
+        bend(3)
+        key(0)
+        gv(3)
+        bend(4)
+        bend(5)
+        key(1)
+        gc("dve" if t else "act", 6, 1)
+        bend(6)
+        gc("dve" if t else "act", 7, 1)
+        bend(7)
+        key(2)
+        if t == 0:
+            consts_mid()
+
+        def dist_x(u):
+            mm(V("PZ%d" % (u % 4), sl(0, 2), sl(0, 256)), V("ID"), V("XV", sl(16 + 512 * u, 528 + 512 * u)), True, False)
+
+        def dist_y(u):
+            pz = "PZ%d" % (u % 4)
+            for k in range(2):
+                c = 2 * u + k
+                mm(V(pz, k, sl(0, 256)), V("YT", sl(128 * (c // 8), 128 * (c // 8) + 128)), V("NBm", sl(256 * (c % 8), 256 * (c % 8) + 256)), False, k == 1)
+            ac(V("Z2", sl(2 * u, 2 * u + 2), sl(0, 224)), V(pz, sl(0, 2), sl(0, 224)), F.Abs)
+
+        def dist_sum(j):
+            o = V("PQ", sl(64 * j, 64 * j + 64))
+            mm(o, V("ID"), V("M2", sl(64 * j, 64 * j + 64)), True, False)
+            mm(o, V("ID"), V("PRE", sl(64 * j, 64 * j + 64)), False, False)
+            for b in range(16):
+                mm(o, V("E", sl(b * 128, b * 128 + 128)), V("Z2", sl(4 * j, 4 * j + 4), sl(b, 256, 16)), False, b == 15)
+
+        dist_x(0)
+        dist_x(1)
+        dist_x(2)
+        key(3)
+        dist_x(3)
+        scan(V("KM"), V("RF"), V("PK", sl(0, 256)), A.mult, A.max)
+        tc(V("KI"), V("KM", sl(15, 256, 16)))
+        ts(V("OFI"), V("KI"), 4095, AND)
+        tc(V("OFU"), V("OFI"))
+        gather("act", V("G3"), V("XC", sl(0, 4096)), V("OFU"))
+        if t == 0:
+            ac(V("Ev"), V("E"), F.Copy, col(7))
+        gather("dve", V("G1"), V("XV", sl(16, 4112)), V("OFU"))
+        gather("dve", V("G2"), V("XV", sl(0, 4096)), V("OFU"))
+        yy = (("G1", "ID"), ("G3", "NEGI"), ("G2", "ID"))
+        for h in range(2):
+            for k, (gm, mat) in enumerate(yy):
+                mm(V("PT", sl(256 + 128 * h, 384 + 128 * h)), V(gm, sl(128 * h, 128 * h + 128)), V(mat), k == 0, k == 2)
+        ts(V("QK"), V("OFI"), 4, SHR, 15, AND)
+        ts(V("YT"), V("PT", sl(256, 512)), 0.0, A.max, 63.0, A.min)
+        for u in range(4):
+            dist_y(u)
+        for k, (gm, mat) in enumerate(yy):
+            mm(V("PT", sl(0, 256)), V(mat), V(gm), k == 0, k == 2)
+        ts(V(ym, sl(0, 256)), V("PT", sl(0, 256)), 0.0, A.max, 63.0, A.min)
+        push(t, ym, "YR" + S, "ay" + S, 1)
+        ts(V("SEEDP", sl(0, 256, 16)), V("QK"), 64.0, A.add)
+        scan(V("SK"), V("RB"), V("SEEDP"), A.mult, A.add)
+        ts(V("PRE"), V("SK"), 1.5, A.is_le, 8192.0, A.mult)
+        if t == 0:
+            ts(V("OF0"), V("QK"), -256.0, A.mult, 3840.0, A.add)
+            tt(V("Ta"), V("OF0"), V("IC"), A.add)
+            tc(V("OFP"), V("Ta"))
+        off = ("OFP", "OFU")[md]
+        gather("dve", V("PG1"), V(cur, sl(16, 4112)), V(off))
+        if t == 0:
+            consts_late()
+        dist_x(4)
+        dist_y(4)
+        small(V("PS", sl(0, 16)), "Ev", "PG1", 256)
+        small(V("PS", sl(16, 32)), "wE", ym, 256)
+        tc(V("UI"), V("PS", sl(16, 32)))
+        ts(V("Td"), V("PS", sl(0, 16)), 37.0, A.mult)
+        ts(V("UI"), V("UI"), 2047, AND)
+        tt(V("SQ"), V("UI"), V("UI"), A.mult)
+        ts(V("SQ"), V("SQ"), 5, SHR)
+        tt(V("HI"), V("SQ"), V("Td"), A.add)
+        ts(V("HI"), V("HI"), 2047, AND)
+        ts(V("HP", sl(0, 16)), V("HI"), 1792, AND)
+        ts(V("HP", sl(16, 32)), V("HI"), 255, AND)
+        tc(V("HHL"), V("HP"))
+        tc(V("HF"), V("HI"))
+        gather("dve", V("PG2"), V(cur, (sl(272, 4368), sl(0, 4096))[md]), V(off))
+        dist_x(5)
+        dist_y(5)
+        dist_sum(0)
+        dist_x(6)
+        dist_y(6)
+        dist_sum(1)
+        dist_x(7)
+        dist_y(7)
+        dist_sum(2)
+        mm(V("PT", sl(256, 512)), V("D01"), V("PG1"), True, False)
+        mm(V("PT", sl(256, 512)), V("S23"), V("PG2"), False, True)
+        dist_sum(3)
+        ts(V("HG"), V("HF"), 1.0, A.add)
+        tt(V("HD"), V("HF"), V("DD"), A.subtract)
+        ts(V("OH"), V("SK"), 0.0, A.is_equal)
+        tt(V("OHT"), V("OH"), V("TPk%d" % md), A.mult)
+        tt(V("OHPP"), V("OHT"), V("POS%d" % md), A.add)
+        ph = V("PQ", sl(256, 512))
+        ts(V(sm, sl(16, 32)), V("QK"), -unit, A.mult, 4096.0 + 16.0 * unit, A.add)
+        ts(V("QM"), V("QK"), -16.0, A.add)
+        ts(V("QN"), V("QK"), 0.0625, A.mult, -4.0, A.add)
+        ts(V("NR"), V("LIVE"), 99.0, A.mult)
+        tt(V("NR"), V("NR"), V("NN"), A.add)
+        o = V("PK", sl(256, 512))
+        mm(o, V("S23"), V("PG1"), True, False)
+        for b in range(16):
+            for k, mat in enumerate(("Rhi", "Rlo")):
+                mm(V("PK", sl(256 + b, 512, 16)), V(mat, sl(b * 128, b * 128 + 128)), V("HHL", sl(16 * k, 16 * k + 16)), False, b == 15 and k == 1)
+        ac(V(cur, sl(8464, 8720)), o)
+        mm(V("PT", sl(0, 256)), V("REPv"), V(cur, sl(8464, 8720)), True, True)
+        ac(V(cur, sl(8208, 8464)), V("PT", sl(256, 512)))
+        if t == 0:
+            ac(V("Ec"), V("E"), F.Copy, col(8))
+        ts(V("NF"), V("PQ", sl(0, 256)), V("lim"), A.is_gt)
+        scan(V("MS"), V("NF"), V("NF"), A.mult, A.add)
+        M = V("MS", sl(15, 256, 16))
+        ts(V("CL"), M, 15.5, A.is_le)
+        tt(V("Ta"), M, V("QM"), A.add)
+        SZ = V(sm, sl(0, 16))
+        tt(SZ, V("Ta"), V("CL"), A.mult)
+        push(t, sm, "SR" + S, "as" + S, 1)
+        tt(V("GR"), V("LIVE"), V("CL"), A.subtract)
+        ts(V("HR"), V("PT", sl(0, 256)), 1.0, A.add)
+
+        def own():
+            ts(V("Tb"), V("GR"), -256.0, A.mult, 320.0, A.add)
+            tt(V("SEEDG", sl(0, 256, 16)), V("Tb"), V("QK"), A.add)
+            tt(V("Ta"), SZ, V("GR"), A.subtract)
+            scan(V("OHG"), V("RB"), V("SEEDG"), A.mult, A.add)
+            ts(V("Tb"), V("Ta"), unit, A.mult)
+            ts(ph, V("OHG"), 1.0, A.is_equal)
+            tt(ph, ph, V("TPn%d" % md), A.mult)
+            tt(V("OHPP"), ph, V("OHPP"), A.add)
+
+        run("dve", lambda e: e.tensor_reduce(V("cls")[0], V("CL")[0], AxisListType.X, A.add), [V("cls")], [V("CL")])
+        tc(V("CLB"), V("cls"))
+        mm(V("PS", sl(64, 65)), V("ONES"), V("CLB"), True, True)
+        dedupe("HR", V("HG"), V("GR"), V("HD"), "OFH", "act", own)
+        tc(V("ci"), V("PS", sl(64, 65)))
+        tt(V("NN"), V("NN"), V("GR"), A.add)
+        xw = V("X", *X_ALL)
+        run("dve", lambda e: e.tensor_copy(xw[0].indirect(V("OFH")[0]), T[ym][:, 0:256]), [xw], [V("OFH"), V(ym, sl(0, 256))])
+        ts(V("ci"), V("ci"), 31, AND)
+        ts(V("NN"), V("NN"), 16.0, A.min)
+        tt(V("lim"), V("ci"), V("thc"), A.add)
+        tt(V("NN"), V("NN"), SZ, A.subtract)
+        if t == 0:
+            consts_last()
+        came(t, "PI", "am")
+        came(t, "YR", "ay")
+        came(t, "SR", "as")
+        if t == 0:
+            iota(V("WIN1", sl(4112, 8208)), [[0, 4096]])
+        for a in range(4):
+            dma("sp", "pi" + S, 64, (T[cur][a:128:16, 4112:8208], cur, 4112, 8208), (T["PI" + S][32 * a:32 * a + 32, :], "PI" + S, 1024 * a, 1024 * a + 1024))
+        sr = V("SR" + S, sl(0, 16))
+        tt(V("TK"), sr, V("NR"), A.is_gt)
+        tt(V("SEEDN", sl(0, 256, 16)), V("QN"), V("TK"), A.add)
+        tt(V("Ta"), V("SR" + S, sl(16, 32)), V("TK"), A.mult)
+        scan(V("SK"), V("RB"), V("SEEDN"), A.mult, A.add)
+        tt(V("SHS", sl(0, 256, 16)), V("Ta"), V("Tb"), A.add)
+        ts(V("GT"), V("SK"), 0.03, A.is_gt)
+        scan(ph, V("GT"), V("SHS"), A.mult, A.add)
+        tt(V("SRC"), V("OHPP"), ph, A.add)
+        ts(V("S0U"), V("SRC", sl(15, 256, 16)), 8703.0, A.min)
+        ts(V("SRCU"), V("SRC"), 8703.0, A.min)
+        win = V(cur, sl(16, 8720))
+        gather("act", V("P0"), win, V("S0U"))
+        mm(V("PT", sl(0, 256)), V("REPv"), V("P0"), True, True)
+        small(V("PS", sl(48, 64)), "Ev", "P0", 256)
+        for j in range(4):
+            gather("act", V(nxt, sl(16 + 1024 * j, 1040 + 1024 * j)), win, V("SRCU", sl(64 * j, 64 * j + 64)))
+        tt(V("Ta"), sr, V("NN"), A.subtract)
+        tt(V("Ta"), V("Ta"), V("TK"), A.mult)
+        tt(V("NN"), V("NN"), V("Ta"), A.add)
+        ts(V("HAS"), V("NN"), 0.5, A.is_ge)
+        tt(V("HAS"), V("HAS"), V("YR" + S, sl(256, 272)), A.mult)
+        ts(V("VR"), V("PT", sl(0, 256)), 1.0, A.add)
+        ts(V("VG"), V("PS", sl(48, 64)), 1.0, A.add)
+        tc(V("V0U"), V("PS", sl(48, 64)))
+        tt(V("HD"), V("PS", sl(48, 64)), V("DD"), A.subtract)
+
+        def blend_in():
+            run("dve", lambda e: e.tensor_tensor(V("BS")[0], T["X"][:, 0:2048].indirect(V("V0U")[0]), T["YR" + S][:, 0:256], A.add),
+                [V("BS")], [V("X", *X_WIN), V("V0U"), V("YR" + S, sl(0, 256))])
+            ts(V("BT"), V("BS"), 0.5, A.mult, 191.75, A.add)
+
+        dedupe("VR", V("VG"), V("HAS"), V("HD"), "OFB", "dve", blend_in)
+        run("dve", lambda e: e.tensor_tensor(xw[0].indirect(V("OFB")[0]), V("BT")[0], V("N192")[0], A.add),
+            [xw], [V("OFB"), V("BT"), V("N192")])
+        for j in range(4):
+            for k, mat in enumerate(("Ev", "Ec")):
+                for b in range(16):
+                    mm(V("PZ%d" % j, k, sl(0, 64)), V(mat, sl(b * 128, b * 128 + 128)), V(nxt, sl(16 + 1024 * j + b, 1040 + 1024 * j, 16)), b == 0, b == 15)
+        if t < ST - 1:
+            start_step(t + 1)
+    dma("sp", "dout", 64, (T["yx"][:], "yx", 0, 1), V("X", sl(0, 2048)))
+    for k, nm in enumerate(("RV0", "RV1", "RS0", "RS1")):
+        ac(V("FD", k, sl(0, 128)), V(nm))
+    ts(V("SEEDS", sl(0, 256, 16)), V("NN"), -15.0, A.add)
+    scan(V("NS"), V("RB"), V("SEEDS"), A.mult, A.add)
+    ts(V("AL"), V("NS"), 0.5, A.is_gt)
+    tc(V("HHL", sl(0, 16)), V("NN"))
+    for j in range(4):
+        h = sl(64 * j, 64 * j + 64)
+        for k, vm in enumerate(("VMV", "VMC")):
+            tt(V(vm, h), V("PZ%d" % j, k, sl(0, 64)), V("AL", h), A.mult)
+    for b in range(16):
+        mm(V("PT", sl(b, 256, 16)), V("Rhi", sl(b * 128, b * 128 + 128)), V("HHL", sl(0, 16)), True, True)
+    ac(V("ON"), V("PT", sl(0, 256)))
+    dma("sp", "dout", 64, (T["yn"][:], "yn", 0, 1), (T["ON"][0:128:16, :], "ON", 0, 256))
+    for k, (vm, y) in enumerate((("VMV", "yv"), ("VMC", "yc"))):
+        run("dve", lambda e: e.transpose(V("FIN")[0], V(vm)[0]), [V("FIN")], [V(vm)])
+        tc(V("FT", sl(0, 8), sl(0, 2), sl(0, 16)), V("FIN"))
+        for eta in range(2):
+            o = V("PZ%d" % k, 0, sl(eta * 128, eta * 128 + 128))
+            mm(o, V("FD", eta, sl(0, 128)), V("FT", sl(0, 8), eta, sl(0, 16)), True, False)
+            mm(o, V("FD", 2 + eta, sl(0, 128)), V("FT", sl(0, 8), 1 - eta, sl(0, 16)), False, True)
+        for eta in range(2):
+            tc(V("FO%d" % k, sl(0, 8), eta, sl(0, 16)), V("PZ%d" % k, 0, sl(eta * 128, eta * 128 + 128)))
+        dma("sp", "dout", 64, (T[y][:], y, 0, 1), V("FO%d" % k, sl(0, 8), sl(0, 2), sl(0, 16)))
+    finish()

@@ -40,12 +40,14 @@ for _n, _w in (("CC", 16), ("KM", 256), ("RF", 256), ("POS0", 256), ("POS1", 256
 _sb("ON", [128, 256], F4)
 for _n, _w in (("VI", 512), ("LNI", 257), ("WTI", 1)):
     _sb(_n, [128, _w], I4)
-for _n, _w in (("VJ", 512), ("VL", 512), ("im", 128), ("imh", 128), ("ip", 1), ("ii", 8),
+for _n, _w in (("WV", 256), ("WC", 256), ("VJ", 512), ("VL", 512), ("im", 128), ("imh", 128), ("ip", 1), ("ii", 8),
                ("J32", 2048), ("KI", 16), ("OFI", 16), ("QK", 16), ("OF0", 16), ("UI", 16), ("SQ", 16), ("HI", 16), ("HP", 32), ("ci", 1)):
     _pack(_n, _w, I4)
 for _n, _w in (("VU", 256), ("CU", 256), ("OFU", 16), ("OFP", 16), ("OFH", 16), ("OFB", 16), ("V0U", 16), ("S0U", 16), ("SRCU", 256),
                ("HR", 256), ("VR", 256)):
     _pack(_n, _w, U2)
+_sb("H16", [128, 16], "float16")
+_sb("Rr", [128, 2048], B2)
 _sb("HL", [128, 4, 8, 2, 16], B2)
 _sb("FT", [128, 8, 2, 16], F4)
 _sb("FO0", [128, 8, 2, 16], F4)
@@ -281,6 +283,7 @@ def rank_program(g, core, T, topo):
     iota(V("RF"), [[0, 16], [1, 16]])
     iota(V("WIN0", sl(0, 4368)), [[0, 4368]])
     iota(V("J32"), [[16, 8], [0, 16], [1, 16]])
+    iota(V("Rlo"), [[0, 2048]])
 
     i_ = lambda k: V("ii", sl(k, k + 1))
     ts(i_(0), V("ip"), 15, AND)
@@ -303,7 +306,8 @@ def rank_program(g, core, T, topo):
         ts(V(nm), V("im"), col(c), A.is_equal, col(h), A.mult)
     tt(col(8), col(8), col(7), A.subtract)
     ts(V("NEG2"), V("im"), col(0), A.is_equal, -2.0, A.mult)
-    fill(V("E"), 0.0)
+    ac(V("E"), V("X", sl(0, 2048)), F.Copy, 0.0)
+    ac(V("Rhi"), V("X", sl(0, 2048)), F.Copy, 0.0)
     for k in range(2):
         h = sl(256 * k, 256 * k + 256)
         ts(V("VJ", h), V("VI", h), 1792, AND)
@@ -335,7 +339,8 @@ def rank_program(g, core, T, topo):
         fill(V("RB", sl(0, 256, 16)), 0.0)
         fill(V("SEEDS"), 1.0)
         lengths_in()
-        start_step(0)
+        for _ in start_step(0):
+            pass
         fill(V("Z", sl(0, 16), sl(0, 32)), 0.0)
         fill(V("Q0T"), 0.0)
         fill(V("Q0T", sl(0, 256, 16)), 16777216.0)
@@ -357,11 +362,7 @@ def rank_program(g, core, T, topo):
         ts(V("NBm"), V("J32"), col(0), A.is_equal, -1.0, A.mult)
         fill(V("Z2", sl(0, 16), sl(224, 256)), 0.0)
         tc(col(9), V("WTI"))
-        fill(V("Rhi"), 0.0)
-        fill(V("Rlo"), 0.0)
-        for k in range(8):
-            tc(V("Rhi", sl(16 * k, 2048, 128)), V("ID", sl(16 * k, 16 * k + 16)))
-            tc(V("Rlo", sl(16 * k + 1, 2048, 128)), V("ID", sl(16 * k, 16 * k + 16)))
+        ts(col(11), col(7), 2048.0, A.mult, col(8), A.add)
 
     def places(m, grow):
         tt(V("OHT"), V("II"), V("POS%d" % m), A.subtract)
@@ -376,6 +377,12 @@ def rank_program(g, core, T, topo):
         fill(V("SEEDG", sl(1, 256, 16)), -65.0)
         fill(V("ZERO"), 0.0)
         fill(V("ONES"), 1.0)
+        ts(V("t1"), V("im", sl(0, 16)), col(1), A.is_equal)
+        for b in range(16):
+            ts(V("Rr", sl(128 * b, 128 * b + 128)), V("BO"), V("t1", sl(b, b + 1)), A.mult)
+        for k in range(8):
+            tc(V("Rhi", sl(16 * k, 2048, 128)), V("ID", sl(16 * k, 16 * k + 16)))
+            tc(V("Rlo", sl(16 * k + 1, 2048, 128)), V("ID", sl(16 * k, 16 * k + 16)))
 
     def consts_last():
         fill(V("SEEDN"), -0.0625)
@@ -399,13 +406,13 @@ def rank_program(g, core, T, topo):
         tc(V("lim"), V("thc"))
 
     def start_step(t):
-        ts(V("LIVE"), V("NN"), 3.5, A.is_ge)
-        tt(V("Tb"), V("NN"), V("LIVE"), A.mult)
-        ts(V("SEEDS", sl(0, 256, 16)), V("Tb"), -15.0, A.add)
-        scan(V("NS"), V("RB"), V("SEEDS"), A.mult, A.add)
-        ts(V("M1"), V("NS"), 3.0, A.is_lt, -16777216.0, A.mult)
-        ts(V("M2"), V("NS"), 0.5, A.is_le, 8192.0, A.mult)
-        tc(V("YM%d" % t, sl(256, 272)), V("LIVE"))
+        yield ts(V("LIVE"), V("NN"), 3.5, A.is_ge)
+        yield tt(V("Tb"), V("NN"), V("LIVE"), A.mult)
+        yield ts(V("SEEDS", sl(0, 256, 16)), V("Tb"), -15.0, A.add)
+        yield scan(V("NS"), V("RB"), V("SEEDS"), A.mult, A.add)
+        yield ts(V("M1"), V("NS"), 3.0, A.is_lt, -16777216.0, A.mult)
+        yield ts(V("M2"), V("NS"), 0.5, A.is_le, 8192.0, A.mult)
+        yield tc(V("YM%d" % t, sl(256, 272)), V("LIVE"))
 
     def push(t, name, out_name, sem, via):
         dst = T.cores[(rank + 1 + t % 7) % len(T.cores)]
@@ -428,19 +435,39 @@ def rank_program(g, core, T, topo):
             if c < 15:
                 mm(V("PT", sl(272 + 16 * c, 512)), V("BO"), V("EQ", c, sl(16, 256 - 16 * c)), False, False)
         d = V("EQ", sl(0, 16), sl(0, 16))
-        tt(d, d, V("PS", sl(256, 512)), A.mult)
-        mm(V("PT", sl(256, 512)), V("BO"), d, False, True)
         tt(V("Te"), vald, act, A.mult)
+        tt(d, d, V("PS", sl(256, 512)), A.mult)
+        if cb != "act":
+            lists_in(0)
+        mm(V("PT", sl(256, 512)), V("BO"), d, False, True)
+        if cb != "act":
+            lists_in(1)
         if cb == "act":
             ac(V("CB"), V("PT", sl(256, 512)))
         else:
             tc(V("CB"), V("PT", sl(256, 512)))
         small(V("PS", sl(32, 48)), "E", "CB", 256)
         meanwhile()
-        ts(V("Td"), V("PS", sl(32, 48)), 0.5, A.is_lt)
-        tt(V("Td"), V("Td"), V("Te"), A.mult)
-        tt(V("t1"), V("Td"), V("DD"), A.add)
-        tc(V(off), V("t1"))
+        yield ts(V("Td"), V("PS", sl(32, 48)), 0.5, A.is_lt)
+        yield tt(V("Td"), V("Td"), V("Te"), A.mult)
+        yield tt(V("t1"), V("Td"), V("DD"), A.add)
+        yield tc(V(off), V("t1"))
+
+    def lists_in(j):
+        nxt = now[0]
+        for b in range(16):
+            mm(V("PZ3" if j > 1 else "PZ0", 0, sl(64 * j, 64 * j + 64)), V("Ec", sl(b * 128, b * 128 + 128)), V(nxt, sl(16 + 1024 * j + b, 1040 + 1024 * j, 16)), b == 0, b == 15)
+
+    now = [None]
+
+    def unpack(k):
+        h = sl(128 * k, 128 * k + 128)
+        w = V(("PZ0", "PZ3")[k], 0, h)
+        yield ts(V("WV", h), w, 2.0 ** -11, A.mult, -0.49976, A.add)
+        yield tc(V("WC", h), w)
+        yield tc(V("VU", h), V("WV", h))
+        yield ts(V("WC", h), V("WC", h), 2047, AND)
+        yield tc(V("CU", h), V("WC", h))
 
     for t in range(ST):
         cur, nxt = "WIN%d" % (t % 2), "WIN%d" % (1 - t % 2)
@@ -449,11 +476,8 @@ def rank_program(g, core, T, topo):
         S = str(t)
         ym, sm = "YM" + S, "SM" + S
 
-        def gv(j):
-            for k in ((0,), (1,), (2, 3), ())[j] if t else ():
-                tc(V("VU", sl(64 * k, 64 * k + 64)), V("PZ%d" % k, 0, sl(0, 64)))
-                tc(V("CU", sl(64 * k, 64 * k + 64)), V("PZ%d" % k, 1, sl(0, 64)))
-            gather("dve", V("XV", sl(16 + 1024 * j, 16 + 1024 * j + 1024)), V("X", *X_WIN), V("VU", sl(64 * j, 64 * j + 64)))
+        def gv(u, n):
+            gather("dve", V("XV", sl(16 + 512 * u, 16 + 512 * u + 512 * n)), V("X", *X_WIN), V("VU", sl(32 * u, 32 * u + 32 * n)))
 
         def gc(q, u, n):
             gather(q, V("XC", sl(512 * u, 512 * u + 512 * n)), V("X", *X_WIN), V("CU", sl(32 * u, 32 * u + 32 * n)))
@@ -479,26 +503,34 @@ def rank_program(g, core, T, topo):
         push(t, "PD" + S, "PI" + S, "am" + S, 0)
         if t == 0:
             iota(V("WIN0", sl(4368, 8208)), [[0, 3840]])
-        gv(0)
-        gc("act", 0, 2)
+        gv(0, 1)
+        gc("act", 0, 1)
         if t == 0:
             consts_early()
-        gv(1)
-        gc("act", 2, 2)
+        gv(1, 1)
+        gc("act", 1, 1)
         bend(0)
+        gc("act", 2, 2)
+        gv(2, 2)
         bend(1)
-        gv(2)
-        gc("act", 4, 2)
         bend(2)
+        if t:
+            st = start_step(t)
+            for _ in unpack(1):
+                next(st)
+            for _ in st:
+                pass
+        gc("act", 4, 2)
+        gv(4, 2)
         bend(3)
+        gc("act", 6, 1)
         key(0)
-        gv(3)
+        gv(6, 2)
         bend(4)
         bend(5)
         key(1)
-        gc("dve" if t else "act", 6, 1)
-        bend(6)
         gc("dve" if t else "act", 7, 1)
+        bend(6)
         bend(7)
         key(2)
         if t == 0:
@@ -560,8 +592,20 @@ def rank_program(g, core, T, topo):
             consts_late()
         dist_x(4)
         dist_y(4)
+        dist_x(5)
+        dist_y(5)
+        dist_sum(0)
         small(V("PS", sl(0, 16)), "Ev", "PG1", 256)
         small(V("PS", sl(16, 32)), "wE", ym, 256)
+        gather("dve", V("PG2"), V(cur, (sl(272, 4368), sl(0, 4096))[md]), V(off))
+        ts(V("OH"), V("SK"), 0.0, A.is_equal)
+        ts(V("NR"), V("LIVE"), 99.0, A.mult)
+        tt(V("OHT"), V("OH"), V("TPk%d" % md), A.mult)
+        tt(V("NR"), V("NR"), V("NN"), A.add)
+        tt(V("OHPP"), V("OHT"), V("POS%d" % md), A.add)
+        ts(V(sm, sl(16, 32)), V("QK"), -unit, A.mult, 4096.0 + 16.0 * unit, A.add)
+        ts(V("QM"), V("QK"), -16.0, A.add)
+        ts(V("QN"), V("QK"), 0.0625, A.mult, -4.0, A.add)
         tc(V("UI"), V("PS", sl(16, 32)))
         ts(V("Td"), V("PS", sl(0, 16)), 37.0, A.mult)
         ts(V("UI"), V("UI"), 2047, AND)
@@ -572,41 +616,31 @@ def rank_program(g, core, T, topo):
         ts(V("HP", sl(0, 16)), V("HI"), 1792, AND)
         ts(V("HP", sl(16, 32)), V("HI"), 255, AND)
         tc(V("HHL"), V("HP"))
+        tc(V("H16"), V("HI"))
         tc(V("HF"), V("HI"))
-        gather("dve", V("PG2"), V(cur, (sl(272, 4368), sl(0, 4096))[md]), V(off))
-        dist_x(5)
-        dist_y(5)
-        dist_sum(0)
+        ts(V("HG"), V("HF"), 1.0, A.add)
+        tt(V("HD"), V("HF"), V("DD"), A.subtract)
         dist_x(6)
         dist_y(6)
         dist_sum(1)
         dist_x(7)
         dist_y(7)
         dist_sum(2)
-        mm(V("PT", sl(256, 512)), V("D01"), V("PG1"), True, False)
-        mm(V("PT", sl(256, 512)), V("S23"), V("PG2"), False, True)
         dist_sum(3)
-        ts(V("HG"), V("HF"), 1.0, A.add)
-        tt(V("HD"), V("HF"), V("DD"), A.subtract)
-        ts(V("OH"), V("SK"), 0.0, A.is_equal)
-        tt(V("OHT"), V("OH"), V("TPk%d" % md), A.mult)
-        tt(V("OHPP"), V("OHT"), V("POS%d" % md), A.add)
+        for b in range(16):
+            mm(V("PT", sl(b, 256, 16)), V("Rr", sl(b * 128, b * 128 + 128)), V("H16"), True, True)
+        ex = V("PK", sl(0, 256))
+        mm(ex, V("D01"), V("PG1"), True, False)
+        mm(ex, V("S23"), V("PG2"), False, True)
         ph = V("PQ", sl(256, 512))
-        ts(V(sm, sl(16, 32)), V("QK"), -unit, A.mult, 4096.0 + 16.0 * unit, A.add)
-        ts(V("QM"), V("QK"), -16.0, A.add)
-        ts(V("QN"), V("QK"), 0.0625, A.mult, -4.0, A.add)
-        ts(V("NR"), V("LIVE"), 99.0, A.mult)
-        tt(V("NR"), V("NR"), V("NN"), A.add)
         o = V("PK", sl(256, 512))
         mm(o, V("S23"), V("PG1"), True, False)
         for b in range(16):
             for k, mat in enumerate(("Rhi", "Rlo")):
                 mm(V("PK", sl(256 + b, 512, 16)), V(mat, sl(b * 128, b * 128 + 128)), V("HHL", sl(16 * k, 16 * k + 16)), False, b == 15 and k == 1)
-        ac(V(cur, sl(8464, 8720)), o)
-        mm(V("PT", sl(0, 256)), V("REPv"), V(cur, sl(8464, 8720)), True, True)
-        ac(V(cur, sl(8208, 8464)), V("PT", sl(256, 512)))
+        ac(V(cur, sl(8208, 8720)), V("PK", sl(0, 512)))
         if t == 0:
-            ac(V("Ec"), V("E"), F.Copy, col(8))
+            ac(V("Ec"), V("E"), F.Copy, col(11))
         ts(V("NF"), V("PQ", sl(0, 256)), V("lim"), A.is_gt)
         scan(V("MS"), V("NF"), V("NF"), A.mult, A.add)
         M = V("MS", sl(15, 256, 16))
@@ -631,14 +665,15 @@ def rank_program(g, core, T, topo):
         run("dve", lambda e: e.tensor_reduce(V("cls")[0], V("CL")[0], AxisListType.X, A.add), [V("cls")], [V("CL")])
         tc(V("CLB"), V("cls"))
         mm(V("PS", sl(64, 65)), V("ONES"), V("CLB"), True, True)
-        dedupe("HR", V("HG"), V("GR"), V("HD"), "OFH", "act", own)
-        tc(V("ci"), V("PS", sl(64, 65)))
+        dd = dedupe("HR", V("HG"), V("GR"), V("HD"), "OFH", "act", own)
+        next(dd)
         tt(V("NN"), V("NN"), V("GR"), A.add)
-        xw = V("X", *X_ALL)
-        run("dve", lambda e: e.tensor_copy(xw[0].indirect(V("OFH")[0]), T[ym][:, 0:256]), [xw], [V("OFH"), V(ym, sl(0, 256))])
-        ts(V("ci"), V("ci"), 31, AND)
+        next(dd)
+        tc(V("ci"), V("PS", sl(64, 65)))
         ts(V("NN"), V("NN"), 16.0, A.min)
-        tt(V("lim"), V("ci"), V("thc"), A.add)
+        xw = V("X", *X_ALL)
+        put = lambda: run("dve", lambda e: e.tensor_copy(xw[0].indirect(V("OFH")[0]), T[ym][:, 0:256]), [xw], [V("OFH"), V(ym, sl(0, 256))])
+        ts(V("ci"), V("ci"), 31, AND)
         tt(V("NN"), V("NN"), SZ, A.subtract)
         if t == 0:
             consts_last()
@@ -651,45 +686,50 @@ def rank_program(g, core, T, topo):
             dma("sp", "pi" + S, 64, (T[cur][a:128:16, 4112:8208], cur, 4112, 8208), (T["PI" + S][32 * a:32 * a + 32, :], "PI" + S, 1024 * a, 1024 * a + 1024))
         sr = V("SR" + S, sl(0, 16))
         tt(V("TK"), sr, V("NR"), A.is_gt)
+        next(dd)
         tt(V("SEEDN", sl(0, 256, 16)), V("QN"), V("TK"), A.add)
         tt(V("Ta"), V("SR" + S, sl(16, 32)), V("TK"), A.mult)
+        next(dd)
         scan(V("SK"), V("RB"), V("SEEDN"), A.mult, A.add)
         tt(V("SHS", sl(0, 256, 16)), V("Ta"), V("Tb"), A.add)
+        tt(V("lim"), V("ci"), V("thc"), A.add)
         ts(V("GT"), V("SK"), 0.03, A.is_gt)
+        tt(V("Ta"), sr, V("NN"), A.subtract)
         scan(ph, V("GT"), V("SHS"), A.mult, A.add)
+        tt(V("Ta"), V("Ta"), V("TK"), A.mult)
         tt(V("SRC"), V("OHPP"), ph, A.add)
+        tt(V("NN"), V("NN"), V("Ta"), A.add)
         ts(V("S0U"), V("SRC", sl(15, 256, 16)), 8703.0, A.min)
         ts(V("SRCU"), V("SRC"), 8703.0, A.min)
+        ts(V("HAS"), V("NN"), 0.5, A.is_ge)
+        put()
         win = V(cur, sl(16, 8720))
         gather("act", V("P0"), win, V("S0U"))
         mm(V("PT", sl(0, 256)), V("REPv"), V("P0"), True, True)
         small(V("PS", sl(48, 64)), "Ev", "P0", 256)
         for j in range(4):
             gather("act", V(nxt, sl(16 + 1024 * j, 1040 + 1024 * j)), win, V("SRCU", sl(64 * j, 64 * j + 64)))
-        tt(V("Ta"), sr, V("NN"), A.subtract)
-        tt(V("Ta"), V("Ta"), V("TK"), A.mult)
-        tt(V("NN"), V("NN"), V("Ta"), A.add)
-        ts(V("HAS"), V("NN"), 0.5, A.is_ge)
         tt(V("HAS"), V("HAS"), V("YR" + S, sl(256, 272)), A.mult)
         ts(V("VR"), V("PT", sl(0, 256)), 1.0, A.add)
         ts(V("VG"), V("PS", sl(48, 64)), 1.0, A.add)
         tc(V("V0U"), V("PS", sl(48, 64)))
         tt(V("HD"), V("PS", sl(48, 64)), V("DD"), A.subtract)
 
+        now[0] = nxt
+
         def blend_in():
             run("dve", lambda e: e.tensor_tensor(V("BS")[0], T["X"][:, 0:2048].indirect(V("V0U")[0]), T["YR" + S][:, 0:256], A.add),
                 [V("BS")], [V("X", *X_WIN), V("V0U"), V("YR" + S, sl(0, 256))])
             ts(V("BT"), V("BS"), 0.5, A.mult, 191.75, A.add)
 
-        dedupe("VR", V("VG"), V("HAS"), V("HD"), "OFB", "dve", blend_in)
+        dd = dedupe("VR", V("VG"), V("HAS"), V("HD"), "OFB", "dve", blend_in)
+        next(dd)
+        for _ in unpack(0):
+            next(dd, None)
         run("dve", lambda e: e.tensor_tensor(xw[0].indirect(V("OFB")[0]), V("BT")[0], V("N192")[0], A.add),
             [xw], [V("OFB"), V("BT"), V("N192")])
-        for j in range(4):
-            for k, mat in enumerate(("Ev", "Ec")):
-                for b in range(16):
-                    mm(V("PZ%d" % j, k, sl(0, 64)), V(mat, sl(b * 128, b * 128 + 128)), V(nxt, sl(16 + 1024 * j + b, 1040 + 1024 * j, 16)), b == 0, b == 15)
-        if t < ST - 1:
-            start_step(t + 1)
+        for j in range(2, 4):
+            lists_in(j)
     dma("sp", "dout", 64, (T["yx"][:], "yx", 0, 1), V("X", sl(0, 2048)))
     for k, nm in enumerate(("RV0", "RV1", "RS0", "RS1")):
         ac(V("FD", k, sl(0, 128)), V(nm))
@@ -697,10 +737,10 @@ def rank_program(g, core, T, topo):
     scan(V("NS"), V("RB"), V("SEEDS"), A.mult, A.add)
     ts(V("AL"), V("NS"), 0.5, A.is_gt)
     tc(V("HHL", sl(0, 16)), V("NN"))
-    for j in range(4):
-        h = sl(64 * j, 64 * j + 64)
-        for k, vm in enumerate(("VMV", "VMC")):
-            tt(V(vm, h), V("PZ%d" % j, k, sl(0, 64)), V("AL", h), A.mult)
+    for _ in unpack(1):
+        pass
+    for w, vm in (("WV", "VMV"), ("WC", "VMC")):
+        tt(V(vm), V(w), V("AL"), A.mult)
     for b in range(16):
         mm(V("PT", sl(b, 256, 16)), V("Rhi", sl(b * 128, b * 128 + 128)), V("HHL", sl(0, 16)), True, True)
     ac(V("ON"), V("PT", sl(0, 256)))

@@ -24,7 +24,7 @@ def _pack(name, width, dtype):
 
 
 for _n, _w in (("X", 2304), ("XV", 4112), ("XC", 4096), ("WIN0", 8720), ("WIN1", 8720), ("E", 2048), ("Ev", 2048), ("Ec", 2048),
-               ("wE", 2048), ("Rhi", 2048), ("Rlo", 2048), ("NBm", 2048), ("ID", 128), ("NEGI", 128), ("NEG2", 128), ("BO", 128),
+               ("wE", 2048), ("Rhi", 2048), ("Rlo", 2048), ("NBm", 2048), ("J32", 2048), ("ID", 128), ("NEGI", 128), ("NEG2", 128), ("BO", 128),
                ("RV0", 128), ("RV1", 128), ("RS0", 128), ("RS1", 128), ("D01", 128), ("S23", 128), ("REPv", 128), ("ONES", 128),
                ("RB", 256), ("SEEDP", 256), ("SEEDG", 256), ("SEEDN", 256), ("SEEDS", 256), ("SHS", 256), ("LChi", 256), ("LClo", 256),
                ("Q0T", 256), ("M1", 256), ("M2", 256), ("PRE", 256), ("SK", 256), ("OH", 256), ("OHG", 256), ("GT", 256), ("SH", 256),
@@ -35,13 +35,13 @@ for _n, _w in (("CC", 16), ("KM", 256), ("RF", 256), ("POS0", 256), ("POS1", 256
                ("TPn0", 256), ("TPn1", 256), ("IC", 16), ("DD", 16), ("OHT", 256), ("OHPP", 256), ("SRC", 256), ("NN", 16), ("LIVE", 16),
                ("NR", 16), ("CL", 16), ("GR", 16), ("Ta", 16), ("Tb", 16), ("Td", 16), ("Te", 16), ("QM", 16), ("QN", 16),
                ("TK", 16), ("HE", 16), ("HF", 16), ("HG", 16), ("HD", 16), ("VG", 16), ("HAS", 16), ("lim", 1), ("thc", 1), ("cls", 1),
-               ("t1", 16), ("FIN", 256), ("VMV", 256), ("VMC", 256), ("AL", 256)):
+               ("t1", 16), ("FIN", 256), ("VMV", 256), ("VMC", 256), ("AL", 256), ("VKS", 256), ("VNS", 256), ("VKT", 256), ("VNT", 256), ("VF", 16), ("Tc", 16)):
     _pack(_n, _w, F4)
 _sb("ON", [128, 256], F4)
 for _n, _w in (("VI", 512), ("LNI", 257), ("WTI", 1)):
     _sb(_n, [128, _w], I4)
-for _n, _w in (("WV", 256), ("WC", 256), ("VJ", 512), ("VL", 512), ("im", 128), ("imh", 128), ("ip", 1), ("ii", 8),
-               ("J32", 2048), ("KI", 16), ("OFI", 16), ("QK", 16), ("OF0", 16), ("UI", 16), ("SQ", 16), ("HI", 16), ("HP", 32), ("ci", 1)):
+for _n, _w in (("WV", 272), ("WC", 256), ("VJ", 512), ("VL", 512), ("im", 128), ("imh", 128), ("ip", 1), ("ii", 8),
+               ("KI", 16), ("OFI", 16), ("QK", 16), ("OF0", 16), ("UI", 16), ("SQ", 16), ("HI", 16), ("HP", 32), ("ci", 1)):
     _pack(_n, _w, I4)
 for _n, _w in (("VU", 256), ("CU", 256), ("OFU", 16), ("OFP", 16), ("OFH", 16), ("OFB", 16), ("V0U", 16), ("S0U", 16), ("SRCU", 256),
                ("HR", 256), ("VR", 256)):
@@ -50,6 +50,8 @@ _sb("H16", [128, 16], "float16")
 _sb("Rr", [128, 2048], B2)
 _sb("HL", [128, 4, 8, 2, 16], B2)
 _sb("FT", [128, 8, 2, 16], F4)
+_sb("FU", [128, 8, 2, 16], F4)
+_sb("HX", [128, 2, 8, 2, 16], "float16")
 _sb("FO0", [128, 8, 2, 16], F4)
 _sb("FO1", [128, 8, 2, 16], F4)
 _sb("FD", [128, 4, 128], F4)
@@ -59,8 +61,8 @@ _sb("Z2", [128, 16, 256], B2)
 for _t in range(ST):
     _sb("YM%d" % _t, [128, 272], B2)
     _sb("YR%d" % _t, [128, 272], B2)
-    _sb("SM%d" % _t, [128, 32], B2)
-    _sb("SR%d" % _t, [128, 32], B2)
+    _sb("SM%d" % _t, [128, 48], F4)
+    _sb("SR%d" % _t, [128, 48], F4)
     _sb("PD%d" % _t, [128, 1024], B2, "dram")
     _sb("PI%d" % _t, [128, 1024], B2, "dram")
 for _t in range(4):
@@ -307,41 +309,49 @@ def rank_program(g, core, T, topo):
     tt(col(8), col(8), col(7), A.subtract)
     ts(V("NEG2"), V("im"), col(0), A.is_equal, -2.0, A.mult)
     ac(V("E"), V("X", sl(0, 2048)), F.Copy, 0.0)
+    for k in range(8):
+        ac(V("E", sl(16 * k, 2048, 129)), V("BO", sl(16 * k, 16 * k + 16)))
     ac(V("Rhi"), V("X", sl(0, 2048)), F.Copy, 0.0)
     for k in range(2):
-        h = sl(256 * k, 256 * k + 256)
-        ts(V("VJ", h), V("VI", h), 1792, AND)
-        ts(V("VL", h), V("VI", h), 255, AND)
-        tc(V("HL", 2 * k, sl(0, 8), sl(0, 2), sl(0, 16)), V("VJ", h))
-        tc(V("HL", 2 * k + 1, sl(0, 8), sl(0, 2), sl(0, 16)), V("VL", h))
-    for a in range(4):
-        dma("sp", "pst", 64, (T["PD0"][32 * a:32 * a + 32, :], "PD0", 1024 * a, 1024 * a + 1024), V("HL", a, sl(0, 8), sl(0, 2), sl(0, 16)))
-    for a in range(4):
-        dma("sp", "po0", 64, (T["WIN0"][a:128:16, 16:4112], "WIN0", 16, 4112), (T["PD0"][32 * a:32 * a + 32, :], "PD0", 1024 * a, 1024 * a + 1024))
+        tc(V("HX", k, sl(0, 8), sl(0, 2), sl(0, 16)), V("VI", sl(256 * k, 256 * k + 256)))
+
+    def payload_in():
+        for k in range(2):
+            h = sl(256 * k, 256 * k + 256)
+            ts(V("VJ", h), V("VI", h), 1792, AND)
+            ts(V("VL", h), V("VI", h), 255, AND)
+            tc(V("HL", 2 * k, sl(0, 8), sl(0, 2), sl(0, 16)), V("VJ", h))
+            tc(V("HL", 2 * k + 1, sl(0, 8), sl(0, 2), sl(0, 16)), V("VL", h))
+        for a in range(4):
+            dma("sp", "pst", 64, (T["PD0"][32 * a:32 * a + 32, :], "PD0", 1024 * a, 1024 * a + 1024), V("HL", a, sl(0, 8), sl(0, 2), sl(0, 16)))
+        for a in range(4):
+            dma("sp", "po0", 64, (T["WIN0"][a:128:16, 16:4112], "WIN0", 16, 4112), (T["PD0"][32 * a:32 * a + 32, :], "PD0", 1024 * a, 1024 * a + 1024))
+
     for k, dst in enumerate(("VU", "CU")):
         pz = "PZ%d" % k
         for kap in range(2):
             o = V(pz, 0, sl(kap * 128, kap * 128 + 128))
-            for n in range(4):
-                part, sw = n // 2, n % 2
-                mm(o, V(("RV%d", "RS%d")[sw] % kap), V("HL", 2 * k + part, sl(0, 8), (kap, 1 - kap)[sw], sl(0, 16)), n == 0, n == 3)
+            for sw in range(2):
+                mm(o, V(("RV%d", "RS%d")[sw] % kap), V("HX", k, sl(0, 8), (kap, 1 - kap)[sw], sl(0, 16)), sw == 0, sw == 1)
         for kap in range(2):
             tc(V("FT", sl(0, 8), kap, sl(0, 16)), V(pz, 0, sl(kap * 128, kap * 128 + 128)))
         tc(V("FIN"), V("FT", sl(0, 8), sl(0, 2), sl(0, 16)))
         run("dve", lambda e: e.transpose(V("VMV")[0], V("FIN")[0]), [V("VMV")], [V("FIN")])
         tc(V(dst), V("VMV"))
+        if k == 0:
+            tc(V("WV", sl(16, 272)), V("VMV"))
+    fill(V("WV", sl(0, 16)), 0)
+    fill(V("Z", sl(0, 16), sl(0, 32)), 0.0)
     fill(V("XV", sl(0, 16)), 0.0)
 
     def consts_early():
-        for k in range(8):
-            tc(V("E", sl(16 * k, 2048, 129)), V("BO", sl(16 * k, 16 * k + 16)))
+        tc(col(9), V("WTI"))
         fill(V("RB"), 1.0)
         fill(V("RB", sl(0, 256, 16)), 0.0)
         fill(V("SEEDS"), 1.0)
         lengths_in()
         for _ in start_step(0):
             pass
-        fill(V("Z", sl(0, 16), sl(0, 32)), 0.0)
         fill(V("Q0T"), 0.0)
         fill(V("Q0T", sl(0, 256, 16)), 16777216.0)
         ts(V("LClo"), V("LClo"), col(1), A.add)
@@ -358,10 +368,8 @@ def rank_program(g, core, T, topo):
         tt(col(10), col(0), col(0), A.subtract)
         ts(col(10), col(10), 2.0, A.add, col(0), A.add)
         ts(V("S23"), V("im"), col(10), A.is_equal, col(7), A.mult)
-        ts(V("REPv"), V("BO"), col(7), A.mult)
         ts(V("NBm"), V("J32"), col(0), A.is_equal, -1.0, A.mult)
         fill(V("Z2", sl(0, 16), sl(224, 256)), 0.0)
-        tc(col(9), V("WTI"))
         ts(col(11), col(7), 2048.0, A.mult, col(8), A.add)
 
     def places(m, grow):
@@ -370,26 +378,17 @@ def rank_program(g, core, T, topo):
         ts(V("TPn%d" % m), V("OHT"), 8448.0 - grow, A.add)
 
     def consts_late():
-        ts(V("wE"), V("E"), col(9), A.mult)
         ts(V("DD"), V("IC"), 2048.0, A.add)
         places(0, -256.0)
         fill(V("SEEDG"), -1.0)
         fill(V("SEEDG", sl(1, 256, 16)), -65.0)
-        fill(V("ZERO"), 0.0)
-        fill(V("ONES"), 1.0)
         ts(V("t1"), V("im", sl(0, 16)), col(1), A.is_equal)
         for b in range(16):
             ts(V("Rr", sl(128 * b, 128 * b + 128)), V("BO"), V("t1", sl(b, b + 1)), A.mult)
-        for k in range(8):
-            tc(V("Rhi", sl(16 * k, 2048, 128)), V("ID", sl(16 * k, 16 * k + 16)))
-            tc(V("Rlo", sl(16 * k + 1, 2048, 128)), V("ID", sl(16 * k, 16 * k + 16)))
 
     def consts_last():
         fill(V("SEEDN"), -0.0625)
         fill(V("SEEDN", sl(1, 256, 16)), 3.9375)
-        fill(V("SHS"), 0.0)
-        fill(V("N192"), -192.0)
-        fill(V("WIN1", sl(0, 16)), 0.0)
         places(1, 16.0)
 
     def lengths_in():
@@ -442,6 +441,9 @@ def rank_program(g, core, T, topo):
         mm(V("PT", sl(256, 512)), V("BO"), d, False, True)
         if cb != "act":
             lists_in(1)
+            if mid[0]:
+                mid[0]()
+                mid[0] = None
         if cb == "act":
             ac(V("CB"), V("PT", sl(256, 512)))
         else:
@@ -458,14 +460,15 @@ def rank_program(g, core, T, topo):
         for b in range(16):
             mm(V("PZ3" if j > 1 else "PZ0", 0, sl(64 * j, 64 * j + 64)), V("Ec", sl(b * 128, b * 128 + 128)), V(nxt, sl(16 + 1024 * j + b, 1040 + 1024 * j, 16)), b == 0, b == 15)
 
-    now = [None]
+    now, mid = [None], [None]
 
     def unpack(k):
         h = sl(128 * k, 128 * k + 128)
         w = V(("PZ0", "PZ3")[k], 0, h)
-        yield ts(V("WV", h), w, 2.0 ** -11, A.mult, -0.49976, A.add)
+        hv = V("WV", sl(h.start + 16, h.stop + 16))
+        yield ts(hv, w, 2.0 ** -11, A.mult, -0.49976, A.add)
         yield tc(V("WC", h), w)
-        yield tc(V("VU", h), V("WV", h))
+        yield tc(V("VU", h), hv)
         yield ts(V("WC", h), V("WC", h), 2047, AND)
         yield tc(V("CU", h), V("WC", h))
 
@@ -500,21 +503,28 @@ def rank_program(g, core, T, topo):
         if t:
             for a in range(4):
                 dma("sp", "po" + S, 64, (T["PD" + S][32 * a:32 * a + 32, :], "PD" + S, 1024 * a, 1024 * a + 1024), (T[cur][a:128:16, 16:4112], cur, 16, 4112))
-        push(t, "PD" + S, "PI" + S, "am" + S, 0)
-        if t == 0:
-            iota(V("WIN0", sl(4368, 8208)), [[0, 3840]])
+            push(t, "PD" + S, "PI" + S, "am" + S, 0)
+        else:
+            iota(V("SHS"), [[0, 256]])
+            iota(V("ZERO"), [[0, 256]])
+            iota(V("ONES"), [[0, 128]], 1)
+            iota(V("N192"), [[0, 256]], -192)
+            iota(V("WIN1", sl(0, 16)), [[0, 16]])
         gv(0, 1)
-        gc("act", 0, 1)
-        if t == 0:
-            consts_early()
         gv(1, 1)
+        if t == 0:
+            payload_in()
+            push(t, "PD" + S, "PI" + S, "am" + S, 0)
+        gc("act", 0, 1)
         gc("act", 1, 1)
-        bend(0)
         gc("act", 2, 2)
         gv(2, 2)
+        bend(0)
         bend(1)
         bend(2)
-        if t:
+        if t == 0:
+            consts_early()
+        else:
             st = start_step(t)
             for _ in unpack(1):
                 next(st)
@@ -534,6 +544,7 @@ def rank_program(g, core, T, topo):
         bend(7)
         key(2)
         if t == 0:
+            ac(V("wE"), V("E"), F.Copy, col(9))
             consts_mid()
 
         def dist_x(u):
@@ -543,7 +554,7 @@ def rank_program(g, core, T, topo):
             pz = "PZ%d" % (u % 4)
             for k in range(2):
                 c = 2 * u + k
-                mm(V(pz, k, sl(0, 256)), V("YT", sl(128 * (c // 8), 128 * (c // 8) + 128)), V("NBm", sl(256 * (c % 8), 256 * (c % 8) + 256)), False, k == 1)
+                mm(V(pz, k, sl(0, 224)), V("YT", sl(128 * (c // 8), 128 * (c // 8) + 128)), V("NBm", sl(256 * (c % 8), 256 * (c % 8) + 224)), False, k == 1)
             ac(V("Z2", sl(2 * u, 2 * u + 2), sl(0, 224)), V(pz, sl(0, 2), sl(0, 224)), F.Abs)
 
         def dist_sum(j):
@@ -563,8 +574,6 @@ def rank_program(g, core, T, topo):
         ts(V("OFI"), V("KI"), 4095, AND)
         tc(V("OFU"), V("OFI"))
         gather("act", V("G3"), V("XC", sl(0, 4096)), V("OFU"))
-        if t == 0:
-            ac(V("Ev"), V("E"), F.Copy, col(7))
         gather("dve", V("G1"), V("XV", sl(16, 4112)), V("OFU"))
         gather("dve", V("G2"), V("XV", sl(0, 4096)), V("OFU"))
         yy = (("G1", "ID"), ("G3", "NEGI"), ("G2", "ID"))
@@ -579,6 +588,8 @@ def rank_program(g, core, T, topo):
             mm(V("PT", sl(0, 256)), V(mat), V(gm), k == 0, k == 2)
         ts(V(ym, sl(0, 256)), V("PT", sl(0, 256)), 0.0, A.max, 63.0, A.min)
         push(t, ym, "YR" + S, "ay" + S, 1)
+        if t == 0:
+            iota(V("WIN0", sl(4368, 8208)), [[0, 3840]])
         ts(V("SEEDP", sl(0, 256, 16)), V("QK"), 64.0, A.add)
         scan(V("SK"), V("RB"), V("SEEDP"), A.mult, A.add)
         ts(V("PRE"), V("SK"), 1.5, A.is_le, 8192.0, A.mult)
@@ -587,27 +598,30 @@ def rank_program(g, core, T, topo):
             tt(V("Ta"), V("OF0"), V("IC"), A.add)
             tc(V("OFP"), V("Ta"))
         off = ("OFP", "OFU")[md]
-        gather("dve", V("PG1"), V(cur, sl(16, 4112)), V(off))
         if t == 0:
             consts_late()
         dist_x(4)
         dist_y(4)
         dist_x(5)
         dist_y(5)
-        dist_sum(0)
-        small(V("PS", sl(0, 16)), "Ev", "PG1", 256)
+        if t == 0:
+            for k in range(8):
+                ac(V("Rhi", sl(16 * k, 2048, 128)), V("ID", sl(16 * k, 16 * k + 16)))
+                ac(V("Rlo", sl(16 * k + 1, 2048, 128)), V("ID", sl(16 * k, 16 * k + 16)))
         small(V("PS", sl(16, 32)), "wE", ym, 256)
-        gather("dve", V("PG2"), V(cur, (sl(272, 4368), sl(0, 4096))[md]), V(off))
-        ts(V("OH"), V("SK"), 0.0, A.is_equal)
-        ts(V("NR"), V("LIVE"), 99.0, A.mult)
-        tt(V("OHT"), V("OH"), V("TPk%d" % md), A.mult)
-        tt(V("NR"), V("NR"), V("NN"), A.add)
-        tt(V("OHPP"), V("OHT"), V("POS%d" % md), A.add)
-        ts(V(sm, sl(16, 32)), V("QK"), -unit, A.mult, 4096.0 + 16.0 * unit, A.add)
+        dist_sum(0)
+        p0 = V("PK", sl(0, 256))
+        ts(p0, V("SK"), 0.0, A.is_equal)
         ts(V("QM"), V("QK"), -16.0, A.add)
-        ts(V("QN"), V("QK"), 0.0625, A.mult, -4.0, A.add)
+        tt(V("VKS"), p0, V("WV", sl(16, 272)), A.mult)
+        tt(V("VNS"), p0, V("WV", sl(15, 271)), A.mult)
+        scan(V("VKT"), V("RF"), V("VKS"), A.mult, A.add)
+        scan(V("VNT"), V("RF"), V("VNS"), A.mult, A.add)
+        tt(V("OHT"), p0, V("TPk%d" % md), A.mult)
+        tc(V(sm, sl(32, 48)), V("VNT", sl(15, 256, 16)))
+        ts(V(sm, sl(16, 32)), V("QK"), -unit, A.mult, 4096.0 + 16.0 * unit, A.add)
         tc(V("UI"), V("PS", sl(16, 32)))
-        ts(V("Td"), V("PS", sl(0, 16)), 37.0, A.mult)
+        ts(V("Td"), V("VKT", sl(15, 256, 16)), 37.0, A.mult)
         ts(V("UI"), V("UI"), 2047, AND)
         tt(V("SQ"), V("UI"), V("UI"), A.mult)
         ts(V("SQ"), V("SQ"), 5, SHR)
@@ -625,6 +639,8 @@ def rank_program(g, core, T, topo):
         dist_sum(1)
         dist_x(7)
         dist_y(7)
+        gather("act", V("PG1"), V(cur, sl(16, 4112)), V(off))
+        gather("act", V("PG2"), V(cur, (sl(272, 4368), sl(0, 4096))[md]), V(off))
         dist_sum(2)
         dist_sum(3)
         for b in range(16):
@@ -658,17 +674,22 @@ def rank_program(g, core, T, topo):
             tt(V("Ta"), SZ, V("GR"), A.subtract)
             scan(V("OHG"), V("RB"), V("SEEDG"), A.mult, A.add)
             ts(V("Tb"), V("Ta"), unit, A.mult)
+            ts(V("NR"), V("LIVE"), 99.0, A.mult)
             ts(ph, V("OHG"), 1.0, A.is_equal)
-            tt(ph, ph, V("TPn%d" % md), A.mult)
-            tt(V("OHPP"), ph, V("OHPP"), A.add)
+            tt(V("OHPP"), V("OHT"), V("POS%d" % md), A.add)
+            tt(V("NR"), V("NR"), V("NN"), A.add)
+            ts(V("QN"), V("QK"), 0.0625, A.mult, -4.0, A.add)
 
-        run("dve", lambda e: e.tensor_reduce(V("cls")[0], V("CL")[0], AxisListType.X, A.add), [V("cls")], [V("CL")])
-        tc(V("CLB"), V("cls"))
-        mm(V("PS", sl(64, 65)), V("ONES"), V("CLB"), True, True)
+            run("dve", lambda e: e.tensor_reduce(V("cls")[0], V("CL")[0], AxisListType.X, A.add), [V("cls")], [V("CL")])
+            tc(V("CLB"), V("cls"))
+            mm(V("PS", sl(64, 65)), V("ONES"), V("CLB"), True, True)
+
         dd = dedupe("HR", V("HG"), V("GR"), V("HD"), "OFH", "act", own)
         next(dd)
+        tt(ph, ph, V("TPn%d" % md), A.mult)
         tt(V("NN"), V("NN"), V("GR"), A.add)
         next(dd)
+        tt(V("OHPP"), ph, V("OHPP"), A.add)
         tc(V("ci"), V("PS", sl(64, 65)))
         ts(V("NN"), V("NN"), 16.0, A.min)
         xw = V("X", *X_ALL)
@@ -686,34 +707,37 @@ def rank_program(g, core, T, topo):
             dma("sp", "pi" + S, 64, (T[cur][a:128:16, 4112:8208], cur, 4112, 8208), (T["PI" + S][32 * a:32 * a + 32, :], "PI" + S, 1024 * a, 1024 * a + 1024))
         sr = V("SR" + S, sl(0, 16))
         tt(V("TK"), sr, V("NR"), A.is_gt)
+        v0 = V("WV", sl(31, 272, 16))
+        tt(V("Tc"), V("SR" + S, sl(32, 48)), v0, A.subtract)
         next(dd)
         tt(V("SEEDN", sl(0, 256, 16)), V("QN"), V("TK"), A.add)
+        tt(V("Tc"), V("Tc"), V("TK"), A.mult)
         tt(V("Ta"), V("SR" + S, sl(16, 32)), V("TK"), A.mult)
-        next(dd)
         scan(V("SK"), V("RB"), V("SEEDN"), A.mult, A.add)
+        tt(V("VF"), v0, V("Tc"), A.add)
         tt(V("SHS", sl(0, 256, 16)), V("Ta"), V("Tb"), A.add)
-        tt(V("lim"), V("ci"), V("thc"), A.add)
         ts(V("GT"), V("SK"), 0.03, A.is_gt)
-        tt(V("Ta"), sr, V("NN"), A.subtract)
+        tc(V("H16"), V("VF"))
         scan(ph, V("GT"), V("SHS"), A.mult, A.add)
-        tt(V("Ta"), V("Ta"), V("TK"), A.mult)
+        tt(V("Ta"), sr, V("NN"), A.subtract)
+        next(dd)
         tt(V("SRC"), V("OHPP"), ph, A.add)
-        tt(V("NN"), V("NN"), V("Ta"), A.add)
-        ts(V("S0U"), V("SRC", sl(15, 256, 16)), 8703.0, A.min)
+        tt(V("Ta"), V("Ta"), V("TK"), A.mult)
+        ts(V("VG"), V("VF"), 1.0, A.add)
         ts(V("SRCU"), V("SRC"), 8703.0, A.min)
+        tt(V("NN"), V("NN"), V("Ta"), A.add)
+        tt(V("HD"), V("VF"), V("DD"), A.subtract)
+        tc(V("V0U"), V("VF"))
         ts(V("HAS"), V("NN"), 0.5, A.is_ge)
-        put()
         win = V(cur, sl(16, 8720))
-        gather("act", V("P0"), win, V("S0U"))
-        mm(V("PT", sl(0, 256)), V("REPv"), V("P0"), True, True)
-        small(V("PS", sl(48, 64)), "Ev", "P0", 256)
+        for b in range(16):
+            mm(V("PT", sl(b, 256, 16)), V("Rr", sl(b * 128, b * 128 + 128)), V("H16"), True, True)
         for j in range(4):
             gather("act", V(nxt, sl(16 + 1024 * j, 1040 + 1024 * j)), win, V("SRCU", sl(64 * j, 64 * j + 64)))
         tt(V("HAS"), V("HAS"), V("YR" + S, sl(256, 272)), A.mult)
         ts(V("VR"), V("PT", sl(0, 256)), 1.0, A.add)
-        ts(V("VG"), V("PS", sl(48, 64)), 1.0, A.add)
-        tc(V("V0U"), V("PS", sl(48, 64)))
-        tt(V("HD"), V("PS", sl(48, 64)), V("DD"), A.subtract)
+        tt(V("lim"), V("ci"), V("thc"), A.add)
+        mid[0] = put
 
         now[0] = nxt
 
@@ -739,19 +763,22 @@ def rank_program(g, core, T, topo):
     tc(V("HHL", sl(0, 16)), V("NN"))
     for _ in unpack(1):
         pass
-    for w, vm in (("WV", "VMV"), ("WC", "VMC")):
-        tt(V(vm), V(w), V("AL"), A.mult)
+    tt(V("VMV"), V("WV", sl(16, 272)), V("AL"), A.mult)
+    tt(V("VMC"), V("WC"), V("AL"), A.mult)
     for b in range(16):
         mm(V("PT", sl(b, 256, 16)), V("Rhi", sl(b * 128, b * 128 + 128)), V("HHL", sl(0, 16)), True, True)
     ac(V("ON"), V("PT", sl(0, 256)))
     dma("sp", "dout", 64, (T["yn"][:], "yn", 0, 1), (T["ON"][0:128:16, :], "ON", 0, 256))
-    for k, (vm, y) in enumerate((("VMV", "yv"), ("VMC", "yc"))):
-        run("dve", lambda e: e.transpose(V("FIN")[0], V(vm)[0]), [V("FIN")], [V(vm)])
-        tc(V("FT", sl(0, 8), sl(0, 2), sl(0, 16)), V("FIN"))
+    fin, ft = ("FIN", "OHT"), ("FT", "FU")
+    for k, vm in enumerate(("VMV", "VMC")):
+        run("dve", lambda e: e.transpose(V(fin[k])[0], V(vm)[0]), [V(fin[k])], [V(vm)])
+    for k in range(2):
+        tc(V(ft[k], sl(0, 8), sl(0, 2), sl(0, 16)), V(fin[k]))
         for eta in range(2):
             o = V("PZ%d" % k, 0, sl(eta * 128, eta * 128 + 128))
-            mm(o, V("FD", eta, sl(0, 128)), V("FT", sl(0, 8), eta, sl(0, 16)), True, False)
-            mm(o, V("FD", 2 + eta, sl(0, 128)), V("FT", sl(0, 8), 1 - eta, sl(0, 16)), False, True)
+            mm(o, V("FD", eta, sl(0, 128)), V(ft[k], sl(0, 8), eta, sl(0, 16)), True, False)
+            mm(o, V("FD", 2 + eta, sl(0, 128)), V(ft[k], sl(0, 8), 1 - eta, sl(0, 16)), False, True)
+    for k, y in enumerate(("yv", "yc")):
         for eta in range(2):
             tc(V("FO%d" % k, sl(0, 8), eta, sl(0, 16)), V("PZ%d" % k, 0, sl(eta * 128, eta * 128 + 128)))
         dma("sp", "dout", 64, (T[y][:], y, 0, 1), V("FO%d" % k, sl(0, 8), sl(0, 2), sl(0, 16)))

import numpy as np
from concourse.mybir import dt, AluOpType as A, AxisListType, ActivationFunctionType as F

ST = 5
B2, F4, I4, U2 = "bfloat16", "float32", "int32", "uint16"
SCRATCH = {}


SHAPE = {}
PLACE = {}


def _sb(name, shape, dtype, where="sbuf"):
    SCRATCH[name] = (where, shape, dtype)
    SHAPE[name] = shape


def _pack(name, width, dtype):
    box = "box_" + dtype
    at = SCRATCH[box][1][1] if box in SCRATCH else 0
    SCRATCH[box] = ("sbuf", [128, at + (width + 15) // 16 * 16], dtype)
    SHAPE[name] = [128, width]
    PLACE[name] = (box, at)


for _n, _w in (("X", 2304), ("XV", 4112), ("XC", 4096), ("WIN0", 8720), ("WIN1", 8720), ("E", 2048), ("Ev", 2048), ("Ec", 2048),
               ("wE", 2048), ("Rhi", 2048), ("Rlo", 2048), ("NBm", 2048), ("J32", 2048), ("ID", 128), ("NEGI", 128), ("NEG2", 128), ("BO", 128),
               ("RV0", 128), ("RV1", 128), ("RS0", 128), ("RS1", 128), ("D01", 128), ("S23", 128), ("REPv", 128), ("ONES", 128),
               ("RB", 256), ("SEEDP", 256), ("SEEDG", 256), ("SEEDN", 256), ("SEEDS", 256), ("SHS", 256), ("LChi", 256), ("LClo", 256),
               ("Q0T", 256), ("M1", 256), ("M2", 256), ("PRE", 256), ("SK", 256), ("OH", 256), ("OHG", 256), ("GT", 256), ("SH", 256),
               ("NS", 256), ("NF", 256), ("MS", 256), ("G1", 256), ("G2", 256), ("G3", 256), ("YT", 256), ("PG1", 256), ("PG2", 256),
               ("P0", 256), ("CB", 256), ("BS", 256), ("BT", 256), ("N192", 256), ("ZERO", 256), ("LNB", 258), ("HHL", 32), ("CLB", 1)):
    (_pack if _w <= 258 else lambda n, w, d: _sb(n, [128, w], d))(_n, _w, B2)
for _n, _w in (("CC", 16), ("KM", 256), ("RF", 256), ("POS0", 256), ("POS1", 256), ("II", 256), ("TPk0", 256), ("TPk1", 256),
               ("TPn0", 256), ("TPn1", 256), ("IC", 16), ("DD", 16), ("OHT", 256), ("OHPP", 256), ("SRC", 256), ("NN", 16), ("LIVE", 16),
               ("NR", 16), ("CL", 16), ("GR", 16), ("Ta", 16), ("Tb", 16), ("Td", 16), ("Te", 16), ("QM", 16), ("QN", 16),
               ("TK", 16), ("HE", 16), ("HF", 16), ("HG", 16), ("HD", 16), ("VG", 16), ("HAS", 16), ("lim", 1), ("thc", 1), ("cls", 1),
               ("t1", 16), ("FIN", 256), ("VMV", 256), ("VMC", 256), ("AL", 256), ("VKS", 256), ("VNS", 256), ("VKT", 256), ("VNT", 256), ("VF", 16), ("Tc", 16)):
    _pack(_n, _w, F4)
_sb("ON", [128, 256], F4)
for _n, _w in (("VI", 512), ("LNI", 257), ("WTI", 1)):
    _sb(_n, [128, _w], I4)
for _n, _w in (("WV", 272), ("WC", 256), ("VJ", 512), ("VL", 512), ("im", 128), ("imh", 128), ("ip", 1), ("ii", 8),
               ("KI", 16), ("OFI", 16), ("QK", 16), ("OF0", 16), ("UI", 16), ("SQ", 16), ("HI", 16), ("HP", 32), ("ci", 1)):
    _pack(_n, _w, I4)
for _n, _w in (("VU", 256), ("CU", 256), ("OFU", 16), ("OFP", 16), ("OFH", 16), ("OFB", 16), ("V0U", 16), ("S0U", 16), ("SRCU", 256),
               ("HR", 256), ("VR", 256)):
    _pack(_n, _w, U2)
_sb("H16", [128, 16], "float16")
_sb("Rr", [128, 2048], B2)
_sb("HL", [128, 4, 8, 2, 16], B2)
_sb("FT", [128, 8, 2, 16], F4)
_sb("FU", [128, 8, 2, 16], F4)
_sb("HX", [128, 2, 8, 2, 16], "float16")
_sb("FO0", [128, 8, 2, 16], F4)
_sb("FO1", [128, 8, 2, 16], F4)
_sb("FD", [128, 4, 128], F4)
_sb("EQ", [128, 16, 256], B2)
_sb("Z", [128, 16, 256], B2)
_sb("Z2", [128, 16, 256], B2)
for _t in range(ST):
    _sb("YM%d" % _t, [128, 272], B2)
    _sb("YR%d" % _t, [128, 272], B2)
    _sb("SM%d" % _t, [128, 48], F4)
    _sb("SR%d" % _t, [128, 48], F4)
    _sb("PD%d" % _t, [128, 1024], B2, "dram")
    _sb("PI%d" % _t, [128, 1024], B2, "dram")
for _t in range(4):
    _sb("PZ%d" % _t, [128, 2, 256], F4, "psum")
for _n in ("PK", "PQ", "PS", "PT"):
    _sb(_n, [128, 512], F4, "psum")
SEMAPHORES = ["q_pe", "q_dve", "q_act", "q_g", "loc", "dv", "dc", "dx", "dln", "dwt", "pst", "dout"]
for _t in range(ST):
    SEMAPHORES += ["po%d" % _t, "pi%d" % _t, "am%d" % _t, "ay%d" % _t, "as%d" % _t]

_RANGE = {}


def _span(name, idx):
    key = name + repr(idx)
    if key not in _RANGE:
        shape = SHAPE[name][1:]
        a = np.arange(int(np.prod(shape))).reshape(shape)[idx]
        _RANGE[key] = (int(a.min()), int(a.max()) + 1)
    return _RANGE[key]


def _queues(g, core, T):
    eng = {"pe": g.tensor, "dve": g.vector, "act": g.scalar, "g": g, "sp": g.sync}
    cnt = {"pe": 0, "dve": 0, "act": 0, "g": 0}
    known = {q: {} for q in eng}
    vc, recs, total = {}, {}, {}

    def V(name, *idx):
        lo, hi = _span(name, idx) if idx else (0, 1 << 20)
        if name in PLACE:
            box, at = PLACE[name]
            k = idx[0] if idx else slice(0, SHAPE[name][1])
            return (T[box][:, at + k.start:at + k.stop:k.step or 1], name, lo, hi)
        return (T[name][(slice(None),) + idx] if idx else T[name][:], name, lo, hi)

    def deps(q, outs, ins, own=None):
        need = {}
        for lst, wr in ((ins, 0), (outs, 1)):
            for (_, name, lo, hi) in lst:
                psum = SCRATCH.get(name, ("",))[0] == "psum"
                for r in recs.get(name, ()):
                    if (q == "pe" and r[4] == "pe") or r[3][0] == own:
                        continue
                    if psum and r[4] != q:
                        hit = True
                    else:
                        hit = r[0] < hi and lo < r[1] and (r[2] or wr)
                    if hit:
                        s, v = r[3]
                        if known[q].get(s, 0) < v and need.get(s, 0) < v:
                            need[s] = v
        for s in sorted(need):
            for s2, v2 in need.items():
                if s2 != s and vc.get((s2, v2), {}).get(s, 0) >= need[s]:
                    need[s] = 0
        for s in sorted(need):
            v = need[s]
            if v:
                eng[q].wait_ge(T.sem[s], v)
                known[q][s] = v
                for s2, v2 in vc.get((s, v), {}).items():
                    if known[q].get(s2, 0) < v2:
                        known[q][s2] = v2

    def note(q, tok, outs, ins):
        for (_, name, lo, hi) in ins:
            l = recs.setdefault(name, [])
            l[:] = [r for r in l if not (not r[2] and r[4] == q and lo <= r[0] and r[1] <= hi)]
            l.append((lo, hi, 0, tok, q))
        for (_, name, lo, hi) in outs:
            l = recs.setdefault(name, [])
            psum = SCRATCH.get(name, ("",))[0] == "psum"
            l[:] = [r for r in l if not (lo <= r[0] and r[1] <= hi) or (psum and r[4] != q)]
            if psum:
                l[:] = [r for r in l if r[4] == q] + [r for r in l if r[4] != q and known[q].get(r[3][0], 0) < r[3][1]]
            l.append((lo, hi, 1, tok, q))

    def run(q, call, outs, ins):
        deps(q, outs, ins)
        cnt[q] += 1
        s = "q_" + q
        call(eng[q]).then_inc(T.sem[s], 1)
        tok = (s, cnt[q])
        d = dict(known[q])
        d[s] = cnt[q]
        vc[tok] = d
        note(q, tok, outs, ins)

    def dma(q, sem, n, out, in_):
        deps(q, [out], [in_], sem)
        eng[q].dma_start(out[0], in_[0]).then_inc(T.sem[sem], 16)
        total[sem] = n
        vc.setdefault((sem, n), dict(known[q]))
        note("dma", (sem, n), [out], [in_])

    def arrive(name, sem, n):
        total[sem] = n
        note("ext", (sem, n), [(None, name, 0, 1 << 20)], [])

    def before(q, ins):
        deps(q, [], ins)

    def finish():
        for q in cnt:
            if cnt[q] and known["g"].get("q_" + q, 0) < cnt[q]:
                g.wait_ge(T.sem["q_" + q], cnt[q])
        for s in sorted(total):
            if known["g"].get(s, 0) < total[s]:
                g.wait_ge(T.sem[s], total[s])

    return V, run, dma, arrive, before, finish, total


def _send(core, T, topo, g, out, in_, arrived, dst):
    e = topo.engines(core, dst)[:8]
    rid, pid = topo.addr(dst, core)
    g.remote_dma(out, in_, T.sem[arrived], T.sem["loc"], pid, rid, sum(1 << k for k in e))
    return len(e)


def _relays(core, dst, topo):
    if topo.may_write(core, dst):
        return []
    c = [k for k in topo.cores_of(core) if k != core and topo.may_write(k, dst)]
    c.sort(key=lambda k: (topo.die(k) != topo.die(core), k))
    return [c[0], c[1 % len(c)]]


def _relay_program(g, core, T, topo):
    loc = 0
    for t in range(ST):
        for r, src in enumerate(T.cores):
            dst = T.cores[(r + 1 + t % 7) % len(T.cores)]
            rl = _relays(src, dst, topo)
            if core not in rl:
                continue
            n = len(topo.engines(src, core)[:8])
            for k, (name, sem) in enumerate((("PI", "am"), ("YR", "ay"), ("SR", "as"))):
                if rl[0 if k == 0 else 1] == core:
                    g.wait_ge(T.sem[sem + str(t)], n)
                    loc += _send(core, T, topo, g, T[name + str(t)][:], T[name + str(t)][:], sem + str(t), dst)
    if loc:
        g.wait_ge(T.sem["loc"], loc)


def rank_program(g, core, T, topo):
    rank = T.rank_of(core)
    if rank is None:
        return _relay_program(g, core, T, topo)
    V, run, dma, arrive, before, finish, total = _queues(g, core, T)
    n_loc = [0]
    sl = slice
    X_ALL, X_WIN = (sl(0, 2304),), (sl(0, 2048),)

    def mm(out, lhsT, rhs, a, z):
        run("pe", lambda e: e.matmul(out[0], lhsT[0], rhs[0], a, z), [out], [lhsT, rhs])

    def ts(out, in0, s1, op0, s2=None, op1=None):
        ins = [in0] + [s for s in (s1, s2) if isinstance(s, tuple)]
        a1 = s1[0] if isinstance(s1, tuple) else s1
        a2 = s2[0] if isinstance(s2, tuple) else s2
        if op1 is None:
            run("dve", lambda e: e.tensor_scalar(out[0], in0[0], a1, None, op0), [out], ins)
        else:
            run("dve", lambda e: e.tensor_scalar(out[0], in0[0], a1, a2, op0, op1), [out], ins)

    def tt(out, a, b, op):
        run("dve", lambda e: e.tensor_tensor(out[0], a[0], b[0], op), [out], [a, b])

    def tc(out, in_):
        run("dve", lambda e: e.tensor_copy(out[0], in_[0]), [out], [in_])

    def ac(out, in_, f=F.Copy, scale=1.0):
        ins = [in_] + ([scale] if isinstance(scale, tuple) else [])
        sc = scale[0] if isinstance(scale, tuple) else scale
        run("act", lambda e: e.activation(out[0], in_[0], f, scale=sc), [out], ins)

    def scan(out, d0, d1, op0, op1):
        run("dve", lambda e: e.tensor_tensor_scan(out[0], d0[0], d1[0], 0.0, op0, op1), [out], [d0, d1])

    def fill(out, c):
        run("dve", lambda e: e.memset(out[0], c), [out], [])

    def iota(out, pattern, base=0, cm=0):
        run("g", lambda e: e.iota(out[0], pattern, base, cm, allow_small_or_imprecise_dtypes=True), [out], [])

    def gather(q, out, win, off):
        ap = win[0].indirect(off[0])
        if q == "act":
            run("act", lambda e: e.activation(out[0], ap, F.Copy), [out], [win, off])
        else:
            run("dve", lambda e: e.tensor_copy(out[0], ap), [out], [win, off])

    def col(k):
        return V("CC", sl(k, k + 1))

    def small(out, mats, rhs_name, n16):
        for b in range(16):
            mm(out, V(mats, sl(b * 128, b * 128 + 128)), V(rhs_name, sl(b, n16, 16)), b == 0, b == 15)

    AND, SHR = A.bitwise_and, A.arith_shift_right

    dma("sp", "dv", 16, V("VI", sl(0, 256)), (T["vl"][:], "vl", 0, 1))
    dma("sp", "dc", 16, V("VI", sl(256, 512)), (T["cl"][:], "cl", 0, 1))
    dma("sp", "dx", 16, V("X", sl(0, 2048)), (T["xc"][:], "xc", 0, 1))
    dma("sp", "dwt", 16, V("WTI"), (T["wt"][:], "wt", 0, 1))
    fill(V("LNI"), 0)
    for out_sl, nm in ((sl(0, 256), "ln"), (sl(256, 257), "th")):
        o = V("LNI", out_sl)
        dma("sp", "dln", 32, (T["LNI"][0:128:16, out_sl], "LNI", o[2], o[3]), (T[nm][:], nm, 0, 1))
    iota(V("im"), [[1, 128]])
    iota(V("ip"), [[0, 1]], 0, 1)
    iota(V("LClo"), [[0, 16], [16, 16]])
    iota(V("LChi"), [[256, 16], [0, 16]])
    iota(V("IC"), [[16, 16]])
    iota(V("II"), [[16, 16], [0, 16]])
    iota(V("POS0"), [[16, 16], [-256, 16]], 3840)
    iota(V("POS1"), [[256, 16], [16, 16]])
    iota(V("RF"), [[0, 16], [1, 16]])
    iota(V("WIN0", sl(0, 4368)), [[0, 4368]])
    iota(V("J32"), [[16, 8], [0, 16], [1, 16]])
    iota(V("Rlo"), [[0, 2048]])

    i_ = lambda k: V("ii", sl(k, k + 1))
    ts(i_(0), V("ip"), 15, AND)
    ts(i_(1), V("ip"), 4, SHR)
    ts(i_(2), V("ip"), 31, AND)
    ts(i_(3), V("ip"), 4, SHR, 1, AND)
    tc(col(0), V("ip"))
    ts(V("imh"), V("im"), 4, SHR)
    tc(V("CC", sl(1, 3)), V("ii", sl(0, 2)))
    tc(col(4), i_(3))
    ts(col(3), i_(3), -1.0, A.mult, 1.0, A.add)
    ts(col(5), i_(0), -2.0, A.mult, 15.0, A.add)
    ts(col(6), i_(2), -2.0, A.mult, 31.0, A.add)
    ts(V("ID"), V("im"), col(0), A.is_equal)
    ts(V("CC", sl(5, 7)), V("CC", sl(5, 7)), col(0), A.add)
    ts(V("BO"), V("imh"), col(2), A.is_equal)
    ts(col(7), i_(0), 1.5, A.is_le)
    ts(col(8), i_(0), 3.5, A.is_le)
    for nm, c, h in (("RV0", 5, 3), ("RV1", 5, 4), ("RS0", 6, 3), ("RS1", 6, 4)):
        ts(V(nm), V("im"), col(c), A.is_equal, col(h), A.mult)
    tt(col(8), col(8), col(7), A.subtract)
    ts(V("NEG2"), V("im"), col(0), A.is_equal, -2.0, A.mult)
    ac(V("E"), V("X", sl(0, 2048)), F.Copy, 0.0)
    for k in range(8):
        ac(V("E", sl(16 * k, 2048, 129)), V("BO", sl(16 * k, 16 * k + 16)))
    ac(V("Rhi"), V("X", sl(0, 2048)), F.Copy, 0.0)
    for k in range(2):
        tc(V("HX", k, sl(0, 8), sl(0, 2), sl(0, 16)), V("VI", sl(256 * k, 256 * k + 256)))

    def payload_in():
        for k in range(2):
            h = sl(256 * k, 256 * k + 256)
            ts(V("VJ", h), V("VI", h), 1792, AND)
            ts(V("VL", h), V("VI", h), 255, AND)
            tc(V("HL", 2 * k, sl(0, 8), sl(0, 2), sl(0, 16)), V("VJ", h))
            tc(V("HL", 2 * k + 1, sl(0, 8), sl(0, 2), sl(0, 16)), V("VL", h))
        for a in range(4):
            dma("sp", "pst", 64, (T["PD0"][32 * a:32 * a + 32, :], "PD0", 1024 * a, 1024 * a + 1024), V("HL", a, sl(0, 8), sl(0, 2), sl(0, 16)))
        for a in range(4):
            dma("sp", "po0", 64, (T["WIN0"][a:128:16, 16:4112], "WIN0", 16, 4112), (T["PD0"][32 * a:32 * a + 32, :], "PD0", 1024 * a, 1024 * a + 1024))

    for k, dst in enumerate(("VU", "CU")):
        pz = "PZ%d" % k
        for kap in range(2):
            o = V(pz, 0, sl(kap * 128, kap * 128 + 128))
            for sw in range(2):
                mm(o, V(("RV%d", "RS%d")[sw] % kap), V("HX", k, sl(0, 8), (kap, 1 - kap)[sw], sl(0, 16)), sw == 0, sw == 1)
        for kap in range(2):
            tc(V("FT", sl(0, 8), kap, sl(0, 16)), V(pz, 0, sl(kap * 128, kap * 128 + 128)))
        tc(V("FIN"), V("FT", sl(0, 8), sl(0, 2), sl(0, 16)))
        run("dve", lambda e: e.transpose(V("VMV")[0], V("FIN")[0]), [V("VMV")], [V("FIN")])
        tc(V(dst), V("VMV"))
        if k == 0:
            tc(V("WV", sl(16, 272)), V("VMV"))
    fill(V("WV", sl(0, 16)), 0)
    fill(V("Z", sl(0, 16), sl(0, 32)), 0.0)
    fill(V("XV", sl(0, 16)), 0.0)

    def consts_early():
        tc(col(9), V("WTI"))
        fill(V("RB"), 1.0)
        fill(V("RB", sl(0, 256, 16)), 0.0)
        fill(V("SEEDS"), 1.0)
        lengths_in()
        for _ in start_step(0):
            pass
        fill(V("Q0T"), 0.0)
        fill(V("Q0T", sl(0, 256, 16)), 16777216.0)
        ts(V("LClo"), V("LClo"), col(1), A.add)

    def consts_mid():
        ts(V("PS", sl(256, 512)), V("RF"), col(1), A.is_gt)
        tc(V("RF"), V("RB"))
        ts(V("NEGI"), V("im"), col(0), A.is_equal, -1.0, A.mult)
        fill(V("SEEDP"), -1.0)
        fill(V("SEEDP", sl(1, 256, 16)), -65.0)
        for nm in ("POS0", "POS1", "II", "IC"):
            ts(V(nm), V(nm), col(1), A.add)
        ts(V("D01"), V("im"), col(0), A.is_equal, col(7), A.mult)
        tt(col(10), col(0), col(0), A.subtract)
        ts(col(10), col(10), 2.0, A.add, col(0), A.add)
        ts(V("S23"), V("im"), col(10), A.is_equal, col(7), A.mult)
        ts(V("NBm"), V("J32"), col(0), A.is_equal, -1.0, A.mult)
        fill(V("Z2", sl(0, 16), sl(224, 256)), 0.0)
        ts(col(11), col(7), 2048.0, A.mult, col(8), A.add)

    def places(m, grow):
        tt(V("OHT"), V("II"), V("POS%d" % m), A.subtract)
        ts(V("TPk%d" % m), V("OHT"), 8192.0, A.add)
        ts(V("TPn%d" % m), V("OHT"), 8448.0 - grow, A.add)

    def consts_late():
        ts(V("DD"), V("IC"), 2048.0, A.add)
        places(0, -256.0)
        fill(V("SEEDG"), -1.0)
        fill(V("SEEDG", sl(1, 256, 16)), -65.0)
        ts(V("t1"), V("im", sl(0, 16)), col(1), A.is_equal)
        for b in range(16):
            ts(V("Rr", sl(128 * b, 128 * b + 128)), V("BO"), V("t1", sl(b, b + 1)), A.mult)

    def consts_last():
        fill(V("SEEDN"), -0.0625)
        fill(V("SEEDN", sl(1, 256, 16)), 3.9375)
        places(1, 16.0)

    def lengths_in():
        tc(V("LNB", sl(0, 256)), V("LNI", sl(0, 256)))
        ts(V("ci"), V("LNI", sl(256, 257)), 1016, AND)
        tc(V("LNB", sl(256, 257)), V("ci"))
        ts(V("ci"), V("LNI", sl(256, 257)), 7, AND)
        tc(V("LNB", sl(257, 258)), V("ci"))
        small(V("PS", sl(80, 96)), "E", "LNB", 256)
        mm(V("PS", sl(96, 97)), V("BO"), V("LNB", sl(256, 257)), True, False)
        mm(V("PS", sl(96, 97)), V("BO"), V("LNB", sl(257, 258)), False, True)
        tc(V("NN"), V("PS", sl(80, 96)))
        tc(V("thc"), V("PS", sl(96, 97)))
        tc(V("lim"), V("thc"))

    def start_step(t):
        yield ts(V("LIVE"), V("NN"), 3.5, A.is_ge)
        yield tt(V("Tb"), V("NN"), V("LIVE"), A.mult)
        yield ts(V("SEEDS", sl(0, 256, 16)), V("Tb"), -15.0, A.add)
        yield scan(V("NS"), V("RB"), V("SEEDS"), A.mult, A.add)
        yield ts(V("M1"), V("NS"), 3.0, A.is_lt, -16777216.0, A.mult)
        yield ts(V("M2"), V("NS"), 0.5, A.is_le, 8192.0, A.mult)
        yield tc(V("YM%d" % t, sl(256, 272)), V("LIVE"))

    def push(t, name, out_name, sem, via):
        dst = T.cores[(rank + 1 + t % 7) % len(T.cores)]
        rl = _relays(core, dst, topo)
        to = rl[via] if rl else dst
        before("g", [V(name)])
        n_loc[0] += _send(core, T, topo, g, T[out_name][:], T[name][:], sem, to)
        total["loc"] = n_loc[0]

    def came(t, name, sem):
        src = T.cores[(rank - 1 - t % 7) % len(T.cores)]
        rl = _relays(src, core, topo)
        arrive(name + str(t), sem + str(t), len(topo.engines(rl[0] if rl else src, core)[:8]))

    def dedupe(vict, val1, act, vald, off, cb, meanwhile):
        tt(V("HE"), val1, act, A.mult)
        mm(V("PT", sl(256, 512)), V("BO"), V("ZERO"), True, False)
        for c in range(16):
            ts(V("EQ", c, sl(0, 256 - 16 * c)), V(vict, sl(16 * c, 256)), V("HE", sl(c, c + 1)), A.is_equal)
            if c < 15:
                mm(V("PT", sl(272 + 16 * c, 512)), V("BO"), V("EQ", c, sl(16, 256 - 16 * c)), False, False)
        d = V("EQ", sl(0, 16), sl(0, 16))
        tt(V("Te"), vald, act, A.mult)
        tt(d, d, V("PS", sl(256, 512)), A.mult)
        if cb != "act":
            lists_in(0)
        mm(V("PT", sl(256, 512)), V("BO"), d, False, True)
        if cb != "act":
            lists_in(1)
            if mid[0]:
                mid[0]()
                mid[0] = None
        if cb == "act":
            ac(V("CB"), V("PT", sl(256, 512)))
        else:
            tc(V("CB"), V("PT", sl(256, 512)))
        small(V("PS", sl(32, 48)), "E", "CB", 256)
        meanwhile()
        yield ts(V("Td"), V("PS", sl(32, 48)), 0.5, A.is_lt)
        yield tt(V("Td"), V("Td"), V("Te"), A.mult)
        yield tt(V("t1"), V("Td"), V("DD"), A.add)
        yield tc(V(off), V("t1"))

    def lists_in(j):
        nxt = now[0]
        for b in range(16):
            mm(V("PZ3" if j > 1 else "PZ0", 0, sl(64 * j, 64 * j + 64)), V("Ec", sl(b * 128, b * 128 + 128)), V(nxt, sl(16 + 1024 * j + b, 1040 + 1024 * j, 16)), b == 0, b == 15)

    now, mid = [None], [None]

    def unpack(k):
        h = sl(128 * k, 128 * k + 128)
        w = V(("PZ0", "PZ3")[k], 0, h)
        hv = V("WV", sl(h.start + 16, h.stop + 16))
        yield ts(hv, w, 2.0 ** -11, A.mult, -0.49976, A.add)
        yield tc(V("WC", h), w)
        yield tc(V("VU", h), hv)
        yield ts(V("WC", h), V("WC", h), 2047, AND)
        yield tc(V("CU", h), V("WC", h))

    for t in range(ST):
        cur, nxt = "WIN%d" % (t % 2), "WIN%d" % (1 - t % 2)
        md = min(t, 1)
        unit = (256.0, -16.0)[md]
        S = str(t)
        ym, sm = "YM" + S, "SM" + S

        def gv(u, n):
            gather("dve", V("XV", sl(16 + 512 * u, 16 + 512 * u + 512 * n)), V("X", *X_WIN), V("VU", sl(32 * u, 32 * u + 32 * n)))

        def gc(q, u, n):
            gather(q, V("XC", sl(512 * u, 512 * u + 512 * n)), V("X", *X_WIN), V("CU", sl(32 * u, 32 * u + 32 * n)))

        def bend(u):
            pz = "PZ%d" % (u % 4)
            for k in range(2):
                o = (2 * u + k) * 256
                for src, mat, a in (("XV", "ID", 16 + o + 32), ("XV", "ID", o + 32), ("XC", "NEG2", o + 32)):
                    mm(V(pz, k, sl(32, 256)), V(mat), V(src, sl(a, a + 224)), a == 16 + o + 32, src == "XC")
            ac(V("Z", sl(2 * u, 2 * u + 2), sl(32, 256)), V(pz, sl(0, 2), sl(32, 256)), F.Abs, 4096.0)

        def key(j):
            o = V("PK", sl(64 * j, 64 * j + 64))
            for k, m in enumerate(("M1", "Q0T", "LChi", "LClo")):
                mm(o, V("ID"), V(m, sl(64 * j, 64 * j + 64)), k == 0, False)
            for b in range(16):
                mm(o, V("E", sl(b * 128, b * 128 + 128)), V("Z", sl(4 * j, 4 * j + 4), sl(b, 256, 16)), False, b == 15)

        if t:
            for a in range(4):
                dma("sp", "po" + S, 64, (T["PD" + S][32 * a:32 * a + 32, :], "PD" + S, 1024 * a, 1024 * a + 1024), (T[cur][a:128:16, 16:4112], cur, 16, 4112))
            push(t, "PD" + S, "PI" + S, "am" + S, 0)
        else:
            iota(V("SHS"), [[0, 256]])
            iota(V("ZERO"), [[0, 256]])
            iota(V("ONES"), [[0, 128]], 1)
            iota(V("N192"), [[0, 256]], -192)
            iota(V("WIN1", sl(0, 16)), [[0, 16]])
        gv(0, 1)
        gv(1, 1)
        if t == 0:
            payload_in()
            push(t, "PD" + S, "PI" + S, "am" + S, 0)
        gc("act", 0, 1)
        gc("act", 1, 1)
        gc("act", 2, 2)
        gv(2, 2)
        bend(0)
        bend(1)
        bend(2)
        if t == 0:
            consts_early()
        else:
            st = start_step(t)
            for _ in unpack(1):
                next(st)
            for _ in st:
                pass
        gc("act", 4, 2)
        gv(4, 2)
        bend(3)
        gc("act", 6, 1)
        key(0)
        gv(6, 2)
        bend(4)
        bend(5)
        key(1)
        gc("dve" if t else "act", 7, 1)
        bend(6)
        bend(7)
        key(2)
        if t == 0:
            ac(V("wE"), V("E"), F.Copy, col(9))
            consts_mid()

        def dist_x(u):
            mm(V("PZ%d" % (u % 4), sl(0, 2), sl(0, 256)), V("ID"), V("XV", sl(16 + 512 * u, 528 + 512 * u)), True, False)

        def dist_y(u):
            pz = "PZ%d" % (u % 4)
            for k in range(2):
                c = 2 * u + k
                mm(V(pz, k, sl(0, 224)), V("YT", sl(128 * (c // 8), 128 * (c // 8) + 128)), V("NBm", sl(256 * (c % 8), 256 * (c % 8) + 224)), False, k == 1)
            ac(V("Z2", sl(2 * u, 2 * u + 2), sl(0, 224)), V(pz, sl(0, 2), sl(0, 224)), F.Abs)

        def dist_sum(j):
            o = V("PQ", sl(64 * j, 64 * j + 64))
            mm(o, V("ID"), V("M2", sl(64 * j, 64 * j + 64)), True, False)
            mm(o, V("ID"), V("PRE", sl(64 * j, 64 * j + 64)), False, False)
            for b in range(16):
                mm(o, V("E", sl(b * 128, b * 128 + 128)), V("Z2", sl(4 * j, 4 * j + 4), sl(b, 256, 16)), False, b == 15)

        dist_x(0)
        dist_x(1)
        dist_x(2)
        key(3)
        dist_x(3)
        scan(V("KM"), V("RF"), V("PK", sl(0, 256)), A.mult, A.max)
        tc(V("KI"), V("KM", sl(15, 256, 16)))
        ts(V("OFI"), V("KI"), 4095, AND)
        tc(V("OFU"), V("OFI"))
        gather("act", V("G3"), V("XC", sl(0, 4096)), V("OFU"))
        gather("dve", V("G1"), V("XV", sl(16, 4112)), V("OFU"))
        gather("dve", V("G2"), V("XV", sl(0, 4096)), V("OFU"))
        yy = (("G1", "ID"), ("G3", "NEGI"), ("G2", "ID"))
        for h in range(2):
            for k, (gm, mat) in enumerate(yy):
                mm(V("PT", sl(256 + 128 * h, 384 + 128 * h)), V(gm, sl(128 * h, 128 * h + 128)), V(mat), k == 0, k == 2)
        ts(V("QK"), V("OFI"), 4, SHR, 15, AND)
        ts(V("YT"), V("PT", sl(256, 512)), 0.0, A.max, 63.0, A.min)
        for u in range(4):
            dist_y(u)
        for k, (gm, mat) in enumerate(yy):
            mm(V("PT", sl(0, 256)), V(mat), V(gm), k == 0, k == 2)
        ts(V(ym, sl(0, 256)), V("PT", sl(0, 256)), 0.0, A.max, 63.0, A.min)
        push(t, ym, "YR" + S, "ay" + S, 1)
        if t == 0:
            iota(V("WIN0", sl(4368, 8208)), [[0, 3840]])
        ts(V("SEEDP", sl(0, 256, 16)), V("QK"), 64.0, A.add)
        scan(V("SK"), V("RB"), V("SEEDP"), A.mult, A.add)
        ts(V("PRE"), V("SK"), 1.5, A.is_le, 8192.0, A.mult)
        if t == 0:
            ts(V("OF0"), V("QK"), -256.0, A.mult, 3840.0, A.add)
            tt(V("Ta"), V("OF0"), V("IC"), A.add)
            tc(V("OFP"), V("Ta"))
        off = ("OFP", "OFU")[md]
        if t == 0:
            consts_late()
        dist_x(4)
        dist_y(4)
        dist_x(5)
        dist_y(5)
        if t == 0:
            for k in range(8):
                ac(V("Rhi", sl(16 * k, 2048, 128)), V("ID", sl(16 * k, 16 * k + 16)))
                ac(V("Rlo", sl(16 * k + 1, 2048, 128)), V("ID", sl(16 * k, 16 * k + 16)))
        small(V("PS", sl(16, 32)), "wE", ym, 256)
        dist_sum(0)
        p0 = V("PK", sl(0, 256))
        ts(p0, V("SK"), 0.0, A.is_equal)
        ts(V("QM"), V("QK"), -16.0, A.add)
        tt(V("VKS"), p0, V("WV", sl(16, 272)), A.mult)
        tt(V("VNS"), p0, V("WV", sl(15, 271)), A.mult)
        scan(V("VKT"), V("RF"), V("VKS"), A.mult, A.add)
        scan(V("VNT"), V("RF"), V("VNS"), A.mult, A.add)
        tt(V("OHT"), p0, V("TPk%d" % md), A.mult)
        tc(V(sm, sl(32, 48)), V("VNT", sl(15, 256, 16)))
        ts(V(sm, sl(16, 32)), V("QK"), -unit, A.mult, 4096.0 + 16.0 * unit, A.add)
        tc(V("UI"), V("PS", sl(16, 32)))
        ts(V("Td"), V("VKT", sl(15, 256, 16)), 37.0, A.mult)
        ts(V("UI"), V("UI"), 2047, AND)
        tt(V("SQ"), V("UI"), V("UI"), A.mult)
        ts(V("SQ"), V("SQ"), 5, SHR)
        tt(V("HI"), V("SQ"), V("Td"), A.add)
        ts(V("HI"), V("HI"), 2047, AND)
        ts(V("HP", sl(0, 16)), V("HI"), 1792, AND)
        ts(V("HP", sl(16, 32)), V("HI"), 255, AND)
        tc(V("HHL"), V("HP"))
        tc(V("H16"), V("HI"))
        tc(V("HF"), V("HI"))
        ts(V("HG"), V("HF"), 1.0, A.add)
        tt(V("HD"), V("HF"), V("DD"), A.subtract)
        dist_x(6)
        dist_y(6)
        dist_sum(1)
        dist_x(7)
        dist_y(7)
        gather("act", V("PG1"), V(cur, sl(16, 4112)), V(off))
        gather("act", V("PG2"), V(cur, (sl(272, 4368), sl(0, 4096))[md]), V(off))
        dist_sum(2)
        dist_sum(3)
        for b in range(16):
            mm(V("PT", sl(b, 256, 16)), V("Rr", sl(b * 128, b * 128 + 128)), V("H16"), True, True)
        ex = V("PK", sl(0, 256))
        mm(ex, V("D01"), V("PG1"), True, False)
        mm(ex, V("S23"), V("PG2"), False, True)
        ph = V("PQ", sl(256, 512))
        o = V("PK", sl(256, 512))
        mm(o, V("S23"), V("PG1"), True, False)
        for b in range(16):
            for k, mat in enumerate(("Rhi", "Rlo")):
                mm(V("PK", sl(256 + b, 512, 16)), V(mat, sl(b * 128, b * 128 + 128)), V("HHL", sl(16 * k, 16 * k + 16)), False, b == 15 and k == 1)
        ac(V(cur, sl(8208, 8720)), V("PK", sl(0, 512)))
        if t == 0:
            ac(V("Ec"), V("E"), F.Copy, col(11))
        ts(V("NF"), V("PQ", sl(0, 256)), V("lim"), A.is_gt)
        scan(V("MS"), V("NF"), V("NF"), A.mult, A.add)
        M = V("MS", sl(15, 256, 16))
        ts(V("CL"), M, 15.5, A.is_le)
        tt(V("Ta"), M, V("QM"), A.add)
        SZ = V(sm, sl(0, 16))
        tt(SZ, V("Ta"), V("CL"), A.mult)
        push(t, sm, "SR" + S, "as" + S, 1)
        tt(V("GR"), V("LIVE"), V("CL"), A.subtract)
        ts(V("HR"), V("PT", sl(0, 256)), 1.0, A.add)

        def own():
            ts(V("Tb"), V("GR"), -256.0, A.mult, 320.0, A.add)
            tt(V("SEEDG", sl(0, 256, 16)), V("Tb"), V("QK"), A.add)
            tt(V("Ta"), SZ, V("GR"), A.subtract)
            scan(V("OHG"), V("RB"), V("SEEDG"), A.mult, A.add)
            ts(V("Tb"), V("Ta"), unit, A.mult)
            ts(V("NR"), V("LIVE"), 99.0, A.mult)
            ts(ph, V("OHG"), 1.0, A.is_equal)
            tt(V("OHPP"), V("OHT"), V("POS%d" % md), A.add)
            tt(V("NR"), V("NR"), V("NN"), A.add)
            ts(V("QN"), V("QK"), 0.0625, A.mult, -4.0, A.add)

            run("dve", lambda e: e.tensor_reduce(V("cls")[0], V("CL")[0], AxisListType.X, A.add), [V("cls")], [V("CL")])
            tc(V("CLB"), V("cls"))
            mm(V("PS", sl(64, 65)), V("ONES"), V("CLB"), True, True)

        dd = dedupe("HR", V("HG"), V("GR"), V("HD"), "OFH", "act", own)
        next(dd)
        tt(ph, ph, V("TPn%d" % md), A.mult)
        tt(V("NN"), V("NN"), V("GR"), A.add)
        next(dd)
        tt(V("OHPP"), ph, V("OHPP"), A.add)
        tc(V("ci"), V("PS", sl(64, 65)))
        ts(V("NN"), V("NN"), 16.0, A.min)
        xw = V("X", *X_ALL)
        put = lambda: run("dve", lambda e: e.tensor_copy(xw[0].indirect(V("OFH")[0]), T[ym][:, 0:256]), [xw], [V("OFH"), V(ym, sl(0, 256))])
        ts(V("ci"), V("ci"), 31, AND)
        tt(V("NN"), V("NN"), SZ, A.subtract)
        if t == 0:
            consts_last()
        came(t, "PI", "am")
        came(t, "YR", "ay")
        came(t, "SR", "as")
        if t == 0:
            iota(V("WIN1", sl(4112, 8208)), [[0, 4096]])
        for a in range(4):
            dma("sp", "pi" + S, 64, (T[cur][a:128:16, 4112:8208], cur, 4112, 8208), (T["PI" + S][32 * a:32 * a + 32, :], "PI" + S, 1024 * a, 1024 * a + 1024))
        sr = V("SR" + S, sl(0, 16))
        tt(V("TK"), sr, V("NR"), A.is_gt)
        v0 = V("WV", sl(31, 272, 16))
        tt(V("Tc"), V("SR" + S, sl(32, 48)), v0, A.subtract)
        next(dd)
        tt(V("SEEDN", sl(0, 256, 16)), V("QN"), V("TK"), A.add)
        tt(V("Tc"), V("Tc"), V("TK"), A.mult)
        tt(V("Ta"), V("SR" + S, sl(16, 32)), V("TK"), A.mult)
        scan(V("SK"), V("RB"), V("SEEDN"), A.mult, A.add)
        tt(V("VF"), v0, V("Tc"), A.add)
        tt(V("SHS", sl(0, 256, 16)), V("Ta"), V("Tb"), A.add)
        ts(V("GT"), V("SK"), 0.03, A.is_gt)
        tc(V("H16"), V("VF"))
        scan(ph, V("GT"), V("SHS"), A.mult, A.add)
        tt(V("Ta"), sr, V("NN"), A.subtract)
        next(dd)
        tt(V("SRC"), V("OHPP"), ph, A.add)
        tt(V("Ta"), V("Ta"), V("TK"), A.mult)
        ts(V("VG"), V("VF"), 1.0, A.add)
        ts(V("SRCU"), V("SRC"), 8703.0, A.min)
        tt(V("NN"), V("NN"), V("Ta"), A.add)
        tt(V("HD"), V("VF"), V("DD"), A.subtract)
        tc(V("V0U"), V("VF"))
        ts(V("HAS"), V("NN"), 0.5, A.is_ge)
        win = V(cur, sl(16, 8720))
        for b in range(16):
            mm(V("PT", sl(b, 256, 16)), V("Rr", sl(b * 128, b * 128 + 128)), V("H16"), True, True)
        for j in range(4):
            gather("act", V(nxt, sl(16 + 1024 * j, 1040 + 1024 * j)), win, V("SRCU", sl(64 * j, 64 * j + 64)))
        tt(V("HAS"), V("HAS"), V("YR" + S, sl(256, 272)), A.mult)
        ts(V("VR"), V("PT", sl(0, 256)), 1.0, A.add)
        tt(V("lim"), V("ci"), V("thc"), A.add)
        mid[0] = put

        now[0] = nxt

        def blend_in():
            run("dve", lambda e: e.tensor_tensor(V("BS")[0], T["X"][:, 0:2048].indirect(V("V0U")[0]), T["YR" + S][:, 0:256], A.add),
                [V("BS")], [V("X", *X_WIN), V("V0U"), V("YR" + S, sl(0, 256))])
            ts(V("BT"), V("BS"), 0.5, A.mult, 191.75, A.add)

        dd = dedupe("VR", V("VG"), V("HAS"), V("HD"), "OFB", "dve", blend_in)
        next(dd)
        for _ in unpack(0):
            next(dd, None)
        run("dve", lambda e: e.tensor_tensor(xw[0].indirect(V("OFB")[0]), V("BT")[0], V("N192")[0], A.add),
            [xw], [V("OFB"), V("BT"), V("N192")])
        for j in range(2, 4):
            lists_in(j)
    dma("sp", "dout", 64, (T["yx"][:], "yx", 0, 1), V("X", sl(0, 2048)))
    for k, nm in enumerate(("RV0", "RV1", "RS0", "RS1")):
        ac(V("FD", k, sl(0, 128)), V(nm))
    ts(V("SEEDS", sl(0, 256, 16)), V("NN"), -15.0, A.add)
    scan(V("NS"), V("RB"), V("SEEDS"), A.mult, A.add)
    ts(V("AL"), V("NS"), 0.5, A.is_gt)
    tc(V("HHL", sl(0, 16)), V("NN"))
    for _ in unpack(1):
        pass
    tt(V("VMV"), V("WV", sl(16, 272)), V("AL"), A.mult)
    tt(V("VMC"), V("WC"), V("AL"), A.mult)
    for b in range(16):
        mm(V("PT", sl(b, 256, 16)), V("Rhi", sl(b * 128, b * 128 + 128)), V("HHL", sl(0, 16)), True, True)
    ac(V("ON"), V("PT", sl(0, 256)))
    dma("sp", "dout", 64, (T["yn"][:], "yn", 0, 1), (T["ON"][0:128:16, :], "ON", 0, 256))
    fin, ft = ("FIN", "OHT"), ("FT", "FU")
    for k, vm in enumerate(("VMV", "VMC")):
        run("dve", lambda e: e.transpose(V(fin[k])[0], V(vm)[0]), [V(fin[k])], [V(vm)])
    for k in range(2):
        tc(V(ft[k], sl(0, 8), sl(0, 2), sl(0, 16)), V(fin[k]))
        for eta in range(2):
            o = V("PZ%d" % k, 0, sl(eta * 128, eta * 128 + 128))
            mm(o, V("FD", eta, sl(0, 128)), V(ft[k], sl(0, 8), eta, sl(0, 16)), True, False)
            mm(o, V("FD", 2 + eta, sl(0, 128)), V(ft[k], sl(0, 8), 1 - eta, sl(0, 16)), False, True)
    for k, y in enumerate(("yv", "yc")):
        for eta in range(2):
            tc(V("FO%d" % k, sl(0, 8), eta, sl(0, 16)), V("PZ%d" % k, 0, sl(eta * 128, eta * 128 + 128)))
        dma("sp", "dout", 64, (T[y][:], y, 0, 1), V("FO%d" % k, sl(0, 8), sl(0, 2), sl(0, 16)))
    finish()
